import numpy as np, ml_dtypes
CORES = [3,11,19,27,35,43,51,59]
N = 8
import mx_ref
BF = ml_dtypes.bfloat16
def entries(a):
    return np.ascontiguousarray(a.T).reshape(-1)
def table(e):
    return np.ascontiguousarray(np.reshape(e, (-1, 16)).T).astype(np.int32)
def pick(q, e):
    c = np.concatenate([q[0].reshape(128, -1, 4), np.zeros((128, 1, 4), np.uint8)], axis=1); s = np.concatenate([q[1], np.ones((16, 1), np.uint8)], axis=1)
    return (np.ascontiguousarray(c[:, e].reshape(128, -1)), np.ascontiguousarray(s[:, e]))
def join(*qs):
    return (np.concatenate([q[0] for q in qs], axis=1), np.concatenate([q[1] for q in qs], axis=1))
def put(q, e, v):
    c, s = q[0].reshape(128, -1, 4).copy(), q[1].copy(); c[:, e] = v[0].reshape(128, -1, 4); s[:, e] = v[1]
    return (c.reshape(128, -1), s)
def pk(c, s):
    return (np.ascontiguousarray(c), mx_ref.live(s))
def emit(q):
    return q[0], q[1]
def packed(v, rng):
    q = [mx_ref.quantize(np.ascontiguousarray(v[r])) for r in range(N)]
    return np.stack([a for a, b in q]), np.stack([mx_ref.plane(b, rng) for a, b in q])
def decode(q):
    o = []
    for b in range(4):
        e = np.zeros((128, 128, 4), np.float32); e[np.arange(128), np.arange(128), b] = 1
        o.append(mx_ref.matmul(mx_ref.quantize(e.reshape(128, 512).astype(BF)), q))
    return np.stack(o, axis=2).reshape(128, -1)
def f(rng, *shape):
    return mx_ref.flush((rng.standard_normal(shape, dtype=np.float32) * np.exp2(rng.integers(-2, 3, shape[:-1] + (1,)))).astype(BF))
def wide(rng, *shape, cols=0):
    v = rng.standard_normal(shape, dtype=np.float32) * np.exp2(rng.integers(-12, 13, shape)).astype(np.float32)
    if cols: v *= np.repeat(np.exp2(rng.integers(-cols, cols + 1, shape[:-2] + (1, shape[-1] // 4))) * (rng.random(shape[:-2] + (1, shape[-1] // 4)) > 0.0625), 4, axis=-1).astype(np.float32)
    return mx_ref.flush(v.astype(BF))
C, S, CAPP = 1024, 256, 48
def big(v, k):
    v = v.astype(np.float32) * np.float32(k)
    v[np.abs(v) < np.float32(2.0 ** -16)] = 0
    return v.astype(BF)
def names(rng, n, each):
    out, at, m = [None] * N, 0, int(n.sum())
    if not each:
        left = np.full(C, 2)
        for s in rng.permutation(N):
            out[s] = rng.permutation(np.flatnonzero(left))[:n[s]]; left[out[s]] -= 1
        return out
    a = rng.permutation(C)[:m // each]
    if each == 2: a = np.concatenate([a, rng.permutation(a)])
    for s in rng.permutation(N):
        out[s] = a[at:at + n[s]]; at += n[s]
    return out
def lists(rng, each=0, full=False, gaps=False, silent=False):
    sn, tc = np.full((N, N * CAPP), -1), np.full((N, N * CAPP), -1)
    n = np.full((N, N), CAPP) if full else rng.integers(CAPP // 4, CAPP, (N, N))
    if gaps: n[:] = CAPP - CAPP // 6
    if silent: n[:, int(rng.integers(0, N))] = 0
    for q in range(N):
        t = names(rng, n[:, q], each)
        for s in range(N): tc[q, s * CAPP + rng.permutation(CAPP)[:n[s, q]]] = t[s]
    for s in range(N):
        used = np.concatenate([tc[q, s * CAPP:s * CAPP + CAPP] >= 0 for q in range(N)])
        e = np.concatenate([rng.permutation(S), rng.integers(0, S, N * CAPP)])[:used.sum()]
        sn[s, used] = rng.permutation(e)
    return {"sn": np.stack([table(v) for v in sn]), "tc": np.stack([table(v) for v in tc])}
def setup_inputs(rng):
    c, p = packed(big(f(rng, N, 128, 4 * C), 1), rng)
    return {"wc": c, "ws": p, "gr": big(f(rng, N, 128, 4 * S), 8), **lists(rng)}
def setup_inputs_cancel(rng):
    tc, P = lists(rng, each=2, full=True, gaps=True)["tc"], S // 2
    x = rng.integers(4, 8, (128, P, 4)) * np.exp2(rng.integers(-2, 1, (128, P, 4))) * rng.choice([-1.0, 1.0], (128, P, 4)) * np.exp2(rng.integers(-2, 3, (128, P, 1)))
    h = rng.integers(0, P, (N, C))
    c, p = packed(np.stack([x[:, h[q]].reshape(128, -1) for q in range(N)]).astype(np.float32).astype(BF), rng)
    g, sn = np.zeros((N, 128, S, 4), np.float32), np.full((N, N * CAPP), -1)
    at = np.stack([rng.permutation(S) for s in range(N)])
    for s in range(N):
        g[s][:, at[s, :P]] = 8 * x
        g[s][:, at[s, P:]] = 8 * x * np.exp2(-rng.integers(21, 25, (P, 1)))
    for q in range(N):
        t = entries(tc[q]).reshape(N, CAPP)
        o = rng.permutation(np.unique(t[t >= 0]))
        late, seen = np.zeros(C, bool), np.zeros(C, bool)
        late[o[:o.size // 2]] = True
        for s in range(N):
            k = np.flatnonzero(t[s] >= 0); e = t[s][k]
            small = seen[e] != late[e]
            sn[s, q * CAPP + k] = at[s][P * small + h[q, e]]
            seen[e] = True
    return {"wc": c, "ws": p, "gr": g.reshape(N, 128, 4 * S).astype(BF), "sn": np.stack([table(v) for v in sn]), "tc": tc}
def setup_inputs_full(rng):
    return {**setup_inputs(rng), **lists(rng, full=True)}
def setup_inputs_most(rng):
    return {**setup_inputs(rng), **lists(rng, each=1, full=True, silent=True)}
def setup_inputs_spread(rng):
    d = setup_inputs(rng)
    d["wc"], d["ws"] = packed(big(wide(rng, N, 128, 4 * C, cols=8), 1), rng)
    d["gr"] = big(wide(rng, N, 128, 4 * S, cols=8), 8)
    return d
def setup_inputs_twice(rng):
    return {**setup_inputs(rng), **lists(rng, each=2, full=True)}
def check_inputs(d):
    b = []
    for r in range(N):
        a, t = entries(d["sn"][r]), entries(d["tc"][r])
        if a.min() < -1 or a.max() >= S: b.append("sn")
        sent = np.concatenate([entries(d["sn"][s])[r * CAPP:r * CAPP + CAPP] for s in range(N)])
        bad = t.min() < -1 or t.max() >= C or ((t >= 0) != (sent >= 0)).any()
        for s in range(N):
            v = t[s * CAPP:s * CAPP + CAPP]; v = v[v >= 0]
            bad = bad or len(set(v.tolist())) != v.size
        if bad or (np.unique(t[t >= 0], return_counts=True)[1] > 2).any(): b.append("tc")
    return b
def reference(wc, ws, gr, sn, tc):
    oc, osc, up = np.zeros((N, 128, 4 * C), np.uint8), np.zeros((N, 16, C), np.uint8), np.zeros((N, 1, C), np.float32)
    g = [decode(mx_ref.quantize(np.ascontiguousarray(gr[s]))).reshape(128, S, 4) for s in range(N)]
    for q in range(N):
        w = pk(wc[q], ws[q])
        v = decode(w).reshape(128, C, 4)
        for s in range(N):
            e, t = entries(sn[s])[q * CAPP:q * CAPP + CAPP], entries(tc[q])[s * CAPP:s * CAPP + CAPP]
            k = t >= 0
            v[:, t[k]] = v[:, t[k]] - g[s][:, e[k]] * np.float32(0.125)
            up[q, 0, t[k]] += 1
        named = np.flatnonzero(up[q, 0])
        new = mx_ref.quantize(np.ascontiguousarray(v.reshape(128, -1).astype(BF)))
        oc[q], osc[q] = emit(put(w, named, pick(new, named)))
    return {"oc": oc, "osc": osc, "up": up}

@@ -1,0 +1,433 @@
+from concourse.bass import DstId, RemoteDMATransfer
+from concourse.mybir import dt, AluOpType as Op, ActivationFunctionType as Fn
+
+C, S, CAP, N = 1024, 256, 48, 8
+KEY = 2048
+NONE = N * KEY
+NEW = 1024
+ZERO = 128
+NA, NB, B0 = 240, 144, 256
+ALL = B0 + NB
+PARTS = (("psa", 0, NA, 0, 16, 32), ("psb", B0, ALL, 32, 42, 52))
+
+E4, U8, F32, I32, U16, BF = "float8_e4m3fn_x4", "uint8", "float32", "int32", "uint16", "bfloat16"
+
+
+def _sb(n, d):
+    return ("sbuf", [128, n], d)
+
+
+SCRATCH = {
+    "grt": _sb(4 * S, BF), "gq": _sb(S, E4), "gs": _sb(S, U8),
+    "snw": _sb(24, I32), "soff": _sb(26, U16),
+    "slotq": _sb(336, E4), "slots": _sb(336, U8),
+    "landq": _sb(ZERO + ALL, E4), "lands": _sb(ZERO + ALL, U8),
+    "zt": _sb(512, BF), "eo": _sb(516, BF), "ef": _sb(516, BF), "en": _sb(516, BF),
+    "eq": _sb(1024, E4), "es": _sb(1024, U8),
+    "wq": _sb(C, E4), "wqs": _sb(C, U8),
+    "finq": _sb(NEW + ZERO + ALL, E4), "fins": _sb(NEW + ZERO + ALL, U8),
+    "wselq": _sb(ALL, E4), "wsels": _sb(ALL, U8),
+    "firq": _sb(ALL, E4), "firs": _sb(ALL, U8),
+    "secq": _sb(ALL, E4), "secs": _sb(ALL, U8),
+    "h": _sb(4 * ALL, BF),
+    "outq": _sb(C, E4), "outs": _sb(C, U8),
+    "tcw": _sb(24, I32), "ta": _sb(24, I32), "tb": _sb(24, I32), "tx": _sb(24, I32), "ty": _sb(24, I32),
+    "tz": _sb(24, I32),
+    "off4": _sb(32, U16), "wl": _sb(26, U16), "fsl": _sb(52, U16), "finl": _sb(64, U16), "upl": _sb(64, U16),
+    "upg": _sb(16, U16),
+    "pidx": _sb(2, I32), "pa": _sb(2, I32), "pcol": _sb(4, F32),
+    "m16": _sb(16, I32), "m16a": _sb(16, I32), "mk": _sb(ALL, F32), "seg": _sb(ALL, F32),
+    "vb": _sb(26, F32), "vw": _sb(26, F32), "cb": _sb(24, F32), "cl": _sb(24, F32),
+    "b48": _sb(48, F32), "vr": _sb(ALL, F32), "tab": _sb(C + CAP, F32), "pv": _sb(ALL, F32),
+    "sc1": _sb(ALL, F32), "sc2": _sb(ALL, F32), "fs": _sb(52, I32), "fa": _sb(52, I32),
+    "tw": _sb(64, F32), "ti": _sb(64, I32), "tf": _sb(64, I32),
+    "hup": _sb(16 + ALL, F32), "upr": _sb(256, F32),
+    "psa": ("psum", [128, 2048], F32), "psb": ("psum", [128, 2048], F32),
+}
+SEMAPHORES = ["vec", "act", "ten", "gpc", "dsn", "dgr", "dtc", "dwc", "dws", "dfin", "dwrap", "dup", "dout",
+              "arrec", "arres", "arrlc", "arrls", "sent", "issued"]
+
+
+def _stages(s):
+    return [(s + i) % N for i in range(1, 5)], [(s + i) % N for i in range(5, N)]
+
+
+def _chain(q):
+    return [(q - 4 + t) % N for t in range(N)]
+
+
+def _engines(s, stage, T, topo):
+    src = T.cores[s]
+    have = len(topo.engines(src, T.cores[stage[0]]))
+    size = 1
+    while 2 * size * len(stage) <= have:
+        size *= 2
+    spare = have - size * len(stage)
+    out, at = {}, 0
+    for q in stage:
+        a, b = topo.chip(src), topo.chip(T.cores[q])
+        n = size
+        if spare >= size and not topo.mates(a, b) and not topo.same_plane(a, b):
+            n, spare = 2 * size, spare - size
+        out[q] = topo.engines(src, T.cores[q])[at:at + n]
+        at += n
+    return out
+
+
+def _pos(t):
+    return CAP * t if t < NA // CAP else CAP * t + B0 - NA
+
+
+def _runs(ranks):
+    out = []
+    for i, r in enumerate(ranks):
+        if out and out[-1][1] + out[-1][2] == r:
+            out[-1][2] += 1
+        else:
+            out.append([i, r, 1])
+    return out
+
+
+def rank_program(g, core, T, topo):
+    me = T.rank_of(core)
+    if me is None:
+        return
+    sem = T.sem
+    ve, sc, te, sy = g.vector, g.scalar, g.tensor, g.sync
+    cnt, seen = {}, {}
+
+    def inc(name, ins, by=1):
+        ins.then_inc(sem[name], by)
+        cnt[name] = cnt.get(name, 0) + by
+        return cnt[name]
+
+    def V(ins):
+        return inc("vec", ins)
+
+    def A(ins):
+        return inc("act", ins)
+
+    def G(ins):
+        return inc("gpc", ins)
+
+    def wait(qn, name, val):
+        if seen.get((qn, name), 0) < val:
+            seen[(qn, name)] = val
+            {"v": ve, "s": sc, "t": te, "y": sy, "g": g}[qn].wait_ge(sem[name], val)
+
+    def iota(out, pattern, base):
+        return G(g.iota(out, pattern, base, 0, allow_small_or_imprecise_dtypes=True))
+
+    one, two = _stages(me)
+    chain = _chain(me)
+    halves = ((0, chain[:5]), (16, chain[5:]))
+    u8, u32 = dt.uint8, dt.uint32
+
+    for k in range(8):
+        inc("dsn", (sc if k < 4 else sy).dma_start(T.snw[16 * k:16 * k + 16, :], T.sn[:]), 16)
+    inc("dgr", sy.dma_start(T.grt[:], T.gr[:]), 16)
+    for k in range(8):
+        inc("dtc", (sc if k < 4 else sy).dma_start(T.tcw[16 * k:16 * k + 16, :], T.tc[:]), 16)
+    inc("dwc", sy.dma_start(T.wq[:].bitcast(u8), T.wc[:]), 16)
+    inc("dws", sc.dma_start(T.wqs[:], T.ws[:]), 16)
+
+    v_eo = V(ve.memset(T.eo[:], 1.0))
+    v_zt = V(ve.memset(T.zt[:], 0.0))
+    p_tab = iota(T.tab[:, 0:64], [[16, 64]], NONE)
+    wait("g", "vec", v_eo)
+    p_ef = G(g.affine_select(T.ef[:], T.eo[:], [[1, 516]], Op.is_equal, 0.0, -3, -4))
+    p_m16 = G(g.iota(T.m16[:], [[1, 16]], 128, -1))
+    p_idx = G(g.iota(T.pidx[:], [[0, 2]], 0, 1))
+    p_cb = iota(T.cb[:], [[0, 8], [16, 3]], C)
+    p_b48 = iota(T.b48[:], [[1, 48]], 0)
+    for base, ranks in halves:
+        for i, r, n in _runs(ranks):
+            c = base + 3 * i
+            p_vb = iota(T.vb[:, c:c + 3 * n], [[KEY + CAP, n], [16, 3]], KEY * r + NEW + ZERO + 16 * c)
+
+    wait("s", "gpc", p_tab)
+    a_tab = 0
+    for r in (1, 2, 4, 8):
+        if a_tab:
+            wait("s", "act", a_tab)
+        a_tab = A(sc.activation(T.tab[:, 64 * r:128 * r], T.tab[:, 0:64 * r], Fn.Identity, bias=float(r)))
+    wait("s", "gpc", p_ef)
+    a_en = A(sc.activation(T.en[:], T.ef[:], Fn.Copy, scale=-0.125))
+    wait("s", "gpc", p_b48)
+    for t, s in enumerate(chain):
+        x = _pos(t)
+        a_vr = A(sc.activation(T.vr[:, x:x + CAP], T.b48[:], Fn.Identity, bias=float(KEY * s + NEW + ZERO + x)))
+
+    V(ve.memset(T.pv[:, 0:CAP], float(NONE)))
+    V(ve.memset(T.pv[:, NA:B0], float(NONE)))
+    V(ve.memset(T.tab[:, C:C + CAP], float(NONE)))
+    V(ve.memset(T.fs[:], 0))
+    v_vb = V(ve.memset(T.vb[:, 15:16], 0.0))
+    V(ve.memset(T.hup[:, 0:16], -3.0))
+    v_seg = V(ve.memset(T.seg[:], 1.0))
+    wait("v", "vec", v_zt)
+    v_zq = V(ve.quantize_mx(T.landq[:, 0:ZERO], T.lands[:, 0:ZERO], T.zt[:]))
+    wait("v", "vec", v_seg)
+    V(ve.memset(T.seg[:, 0:ALL:16], 0.0))
+
+    def unit(k, src):
+        b = k % 4
+        return V(ve.quantize_mx(T.eq[:, 128 * k:128 * k + 128], T.es[:, 128 * k:128 * k + 128],
+                                src[:, 3 - b:3 - b + 512]))
+
+    wait("v", "gpc", p_ef)
+    for k in range(4):
+        v_ep = unit(k, T.ef)
+    wait("v", "gpc", p_m16)
+    v = V(ve.tensor_scalar(T.m16a[:], T.m16[:], 15, None, Op.bitwise_and))
+    wait("v", "gpc", p_idx)
+    v_pa = V(ve.tensor_scalar(T.pa[:], T.pidx[:], 15, None, Op.bitwise_and))
+    wait("v", "vec", v)
+    v_mk = V(ve.tensor_scalar(T.mk[:, 0:16], T.m16a[:], 0.0, None, Op.is_equal))
+    wait("v", "vec", v_pa)
+    v_pc = V(ve.tensor_copy(T.pcol[:, 0:1], T.pa[:, 0:1]))
+
+    wait("v", "dsn", cnt["dsn"])
+    for base, ranks in ((0, one), (12, two), (22, [me])):
+        for i, r, n in _runs(ranks):
+            V(ve.tensor_copy(T.soff[:, base + 3 * i:base + 3 * (i + n)], T.snw[:, 3 * r:3 * (r + n)]))
+    wait("v", "gpc", p_cb)
+    wait("v", "vec", v_pc)
+    v_cl = V(ve.tensor_scalar(T.cl[:], T.cb[:], T.pcol[:, 0:1], None, Op.add))
+    wait("v", "dgr", cnt["dgr"])
+    v_gq = V(ve.quantize_mx(T.gq[:], T.gs[:], T.grt[:]))
+
+    def pickc(out, a, b, win, w0, w1, off, o0, o1):
+        return V(ve.tensor_copy(out[:, a:b].bitcast(u32), win[:, w0:w1].bitcast(u32).indirect(off[:, o0:o1])))
+
+    def picks(out, a, b, win, w0, w1, off, o0, o1):
+        return A(sc.activation(out[:, a:b], win[:, w0:w1].indirect(off[:, o0:o1]), Fn.Copy))
+
+    wait("v", "vec", v_gq)
+    wait("s", "vec", v_gq)
+    n1, n2 = CAP * len(one), CAP * (len(one) + len(two))
+    own = ZERO + _pos(chain.index(me))
+    v_p1 = pickc(T.slotq, 0, n1, T.gq, 0, S, T.soff, 0, 12)
+    a_p1 = picks(T.slots, 0, n1, T.gs, 0, S, T.soff, 0, 12)
+    wait("v", "dtc", cnt["dtc"])
+    v_ta = V(ve.tensor_scalar(T.ta[:], T.tcw[:], 15, None, Op.bitwise_and))
+    v_p2 = pickc(T.slotq, n1, n2, T.gq, 0, S, T.soff, 12, 21)
+    a_p2 = picks(T.slots, n1, n2, T.gs, 0, S, T.soff, 12, 21)
+    V(ve.tensor_scalar(T.tb[:], T.tcw[:], 2047, 4, Op.bitwise_and, Op.logical_shift_right))
+    wait("v", "vec", v_ta)
+    v_tx = V(ve.tensor_scalar(T.tx[:], T.ta[:], 64.0, None, Op.mult))
+    v_own = pickc(T.landq, own, own + CAP, T.gq, 0, S, T.soff, 22, 25)
+    a_own = picks(T.lands, own, own + CAP, T.gs, 0, S, T.soff, 22, 25)
+    wait("v", "vec", v_tx)
+    v_ty = V(ve.tensor_tensor(T.ty[:], T.tx[:], T.tb[:], Op.add))
+
+    sent = 0
+    for stage, a, vp, ap, cs, ss in ((one, 0, v_p1, a_p1, "arrec", "arres"), (two, n1, v_p2, a_p2, "arrlc", "arrls")):
+        eng = _engines(me, stage, T, topo)
+        for codes in (True, False):
+            wait("g", "vec" if codes else "act", vp if codes else ap)
+            tr = []
+            for i, q in enumerate(stage):
+                rid, pid, _se = topo.addr(T.cores[q])
+                x = a + CAP * i
+                y = ZERO + _pos(_chain(q).index(me))
+                src, dst = ((T.slotq[:, x:x + CAP].bitcast(u8), T.landq[:, y:y + CAP].bitcast(u8)) if codes
+                            else (T.slots[:, x:x + CAP], T.lands[:, y:y + CAP]))
+                tr.append(RemoteDMATransfer(dst_ids=[DstId(rid=rid, pnc=pid)],
+                                            dma_engine_mask=sum(1 << e for e in eng[q]),
+                                            remote_sem=sem[cs if codes else ss], src=src, dst=dst))
+                sent += len(eng[q])
+            g.remote_dma_fused(tr, local_sem=sem["sent"])
+    g.sem_inc(sem["issued"], 1)
+
+    wait("y", "issued", 1)
+    inc("dfin", sy.dma_start(T.finq[:, 0:C // 2].bitcast(u8), T.wc[:, 0:2 * C]), 16)
+
+    wait("s", "vec", v_mk)
+    a_mk, n = 0, 16
+    while n < ALL:
+        m = min(n, ALL - n)
+        if a_mk:
+            wait("s", "act", a_mk)
+        a_mk = A(sc.activation(T.mk[:, n:n + m], T.mk[:, 0:m], Fn.Copy))
+        n += m
+    wait("s", "gpc", p_vb)
+    wait("s", "vec", max(v_pc, v_vb))
+    a_vw = A(sc.activation(T.vw[:, 0:25], T.vb[:, 0:25], Fn.Identity, bias=T.pcol[:, 0:1]))
+
+    late, todo = {}, []
+
+    def do_wl(a, b, x, y):
+        late["wl"] = V(ve.tensor_copy(T.wl[:, a:b], T.tcw[:, x:y]))
+
+    def do_em(k):
+        wait("v", "act", a_en)
+        late["em"] = unit(k, T.en)
+
+    def do_w(a, b):
+        wait("v", "dwc", cnt["dwc"])
+        wait("v", "vec", late["wl"])
+        wait("s", "dws", cnt["dws"])
+        wait("s", "vec", late["wl"])
+        late["w"] = pickc(T.wselq, a, b, T.wq, 0, C, T.wl, a // 16, b // 16)
+        late["ws"] = picks(T.wsels, a, b, T.wqs, 0, C, T.wl, a // 16, b // 16)
+
+    def do_list(part, step):
+        _ps, a, z, x, y, e = part
+        key, n = ("list", a), (z - a) // 16
+        if step == 0:
+            wait("v", "act", a_mk)
+            wait("v", "vec", late["pv"])
+            late[key] = V(ve.tensor_tensor_scan(T.sc1[:, a:z], T.pv[:, a:z], T.mk[:, a:z], 0.0, Op.add, Op.mult))
+            return
+        wait("v", "vec", late[key])
+        if step == 1:
+            late[key] = V(ve.tensor_tensor_scan(T.sc2[:, a:z], T.seg[:, a:z], T.sc1[:, a:z], 0.0, Op.mult, Op.add))
+        elif step == 2:
+            wait("v", "act", a_vw)
+            gw, mine = T.sc2[:, a + 15:z:16], T.vw[:, a // 16:z // 16]
+            V(ve.tensor_tensor(T.fs[:, x:x + n], mine, gw, Op.min))
+            late[key] = V(ve.tensor_tensor(T.fs[:, y:y + n], mine, gw, Op.max))
+        elif step == 3:
+            late[key] = V(ve.tensor_scalar(T.fa[:, x:e], T.fs[:, x:e], KEY - 1, None, Op.bitwise_and))
+        else:
+            late[key] = V(ve.tensor_scalar(T.fsl[:, x:e], T.fa[:, x:e], float(NEW), float(NEW), Op.max, Op.subtract))
+
+    for base, ranks in halves:
+        for i, r, n in _runs(ranks):
+            todo.append((do_wl, (base + 3 * i, base + 3 * (i + n), 3 * r, 3 * (r + n))))
+    for k in range(4, 8):
+        todo.append((do_em, (k,)))
+    todo.append((do_w, (0, NA)))
+    todo.append((do_w, (B0, ALL)))
+
+    def filler(n=1):
+        for _i in range(n):
+            if todo:
+                f, args = todo.pop(0)
+                f(*args)
+
+    filler()
+    wait("v", "vec", max(v_ty, v_cl))
+    v_tz = V(ve.tensor_tensor(T.tz[:], T.ty[:], T.cl[:], Op.min))
+    filler()
+    wait("v", "vec", v_tz)
+    for i in range(3):
+        v_off = V(ve.tensor_copy(T.off4[:, i:32:4], T.tz[:, i:24:3]))
+    filler()
+    wait("v", "act", max(a_tab, a_vr))
+    wait("v", "vec", v_off)
+    v_sc = 0
+    for t, s in enumerate(chain):
+        x = _pos(t)
+        win = T.tab[:, 0:C + CAP]
+        off = T.off4[:, 4 * s:4 * s + 3]
+        if t:
+            wait("v", "vec", v_sc)
+            late["pv"] = V(ve.tensor_copy(T.pv[:, x:x + CAP], win.indirect(off)))
+            if t == 4:
+                filler(len(todo))
+                todo.extend((do_list, (PARTS[0], k)) for k in range(5))
+            else:
+                filler()
+            wait("v", "vec", late["pv"])
+        v_sc = V(ve.tensor_copy(win.indirect(off), T.vr[:, x:x + CAP]))
+        if t:
+            filler()
+    filler(len(todo))
+    wait("y", "vec", v_sc)
+    for k in range(8):
+        inc("dwrap", sy.dma_start(T.tw[16 * k:16 * k + 16, :], T.tab[16 * k:16 * k + 1, 0:C]), 16)
+    inc("dfin", sy.dma_start(T.finq[:, C // 2:C].bitcast(u8), T.wc[:, 2 * C:4 * C]), 16)
+    inc("dfin", sy.dma_start(T.fins[:, 0:C], T.ws[:]), 16)
+    for k in range(5):
+        do_list(PARTS[1], k)
+    wait("s", "vec", late["pv"])
+    a_h = A(sc.activation(T.hup[:, 16:16 + ALL], T.pv[:], Fn.Sign, bias=float(NONE - KEY // 8), scale=-1.0))
+
+    def prod(ps, b, k, q, s, a, z, start, stop):
+        return te.matmul_mx(T[ps][:, 512 * b:512 * b + z - a], T.eq[:, 128 * k:128 * k + 128],
+                            T.es[:, 128 * k:128 * k + 128], T[q][:, a:z], T[s][:, a:z], start, stop)
+
+    wait("t", "vec", max(late["w"], v_ep))
+    wait("t", "act", late["ws"])
+    for ps, a, z, _x, _y, _e in PARTS:
+        for b in range(4):
+            prod(ps, b, b, "wselq", "wsels", a, z, True, False)
+
+    def arrived(stage):
+        return sum(len(_engines(s, _stages(s)[stage], T, topo)[me])
+                   for s in range(N) if s != me and me in _stages(s)[stage])
+
+    stops = []
+    for i, (ps, a, z, x, y, e) in enumerate(PARTS):
+        w1, n = ZERO + z, (z - a) // 16
+        wait("v", "arrec" if i == 0 else "arrlc", arrived(i))
+        wait("s", "arres" if i == 0 else "arrls", arrived(i))
+        wait("v", "vec", max(late["list", a], v_own, v_zq))
+        wait("s", "vec", max(late["list", a], v_zq))
+        wait("s", "act", a_own)
+        for q, s, o, last in (("firq", "firs", x, False), ("secq", "secs", y, True)):
+            vp = pickc(T[q], a, z, T.landq, 0, w1, T.fsl, o, o + n)
+            ap = picks(T[s], a, z, T.lands, 0, w1, T.fsl, o, o + n)
+            wait("t", "vec", max(vp, late["em"]))
+            wait("t", "act", ap)
+            for b in range(4):
+                ins = prod(ps, b, 4 + b, q, s, a, z, False, last)
+                if last:
+                    stops.append(inc("ten", ins))
+
+    wait("v", "dwrap", cnt["dwrap"])
+    v_ti = V(ve.tensor_copy(T.ti[:], T.tw[:]))
+
+    for i, (ps, a, z, _x, _y, _e) in enumerate(PARTS):
+        vl = al = 0
+        for b in range(4):
+            out, src = T.h[:, 4 * a + b:4 * z:4], T[ps][:, 512 * b:512 * b + z - a]
+            if b % 2 == 0:
+                wait("v", "ten", stops[4 * i + b])
+                vl = V(ve.tensor_copy(out, src))
+                if i == 0 and b == 0:
+                    wait("v", "vec", v_ti)
+                    v_tf = V(ve.tensor_scalar(T.tf[:], T.ti[:], KEY - 1, None, Op.bitwise_and))
+            else:
+                wait("s", "ten", stops[4 * i + b])
+                al = A(sc.activation(out, src, Fn.Copy))
+        if i == 0:
+            wait("v", "vec", v_tf)
+            v_up = V(ve.tensor_scalar(T.upl[:], T.tf[:], float(NEW + ZERO - 16), float(NEW + ZERO - 16),
+                                      Op.max, Op.subtract))
+            v_fin = V(ve.tensor_copy(T.finl[:], T.tf[:]))
+        wait("v", "vec", vl)
+        wait("v", "act", al)
+        x = NEW + ZERO
+        v_q = V(ve.quantize_mx(T.finq[:, x + a:x + z], T.fins[:, x + a:x + z], T.h[:, 4 * a:4 * z]))
+
+    wait("y", "vec", v_up)
+    for k in range(8):
+        c = 16 * (k // 2)
+        inc("dup", sy.dma_start(T.upg[16 * k:16 * k + 16, :], T.upl[16 * k:16 * k + 16, c:c + 16]), 16)
+
+    wait("v", "vec", max(v_q, v_fin))
+    wait("v", "dfin", cnt["dfin"])
+    wait("s", "vec", max(v_q, v_fin))
+    wait("s", "dfin", cnt["dfin"])
+    W = NEW + ZERO + ALL
+    for j in range(4):
+        vp = pickc(T.outq, 256 * j, 256 * j + 256, T.finq, 0, W, T.finl, 16 * j, 16 * j + 16)
+        ap = picks(T.outs, 256 * j, 256 * j + 256, T.fins, 0, W, T.finl, 16 * j, 16 * j + 16)
+        wait("y", "vec", vp)
+        inc("dout", sy.dma_start(T.oc[:, 1024 * j:1024 * j + 1024], T.outq[:, 256 * j:256 * j + 256].bitcast(u8)), 16)
+    wait("y", "act", ap)
+    for k in range(4):
+        inc("dout", sy.dma_start(T.osc[4 * k:4 * k + 4, :], T.outs[32 * k:32 * k + 4, :]), 16)
+    wait("s", "dup", cnt["dup"])
+    wait("s", "act", a_h)
+    a_up = A(sc.activation(T.upr[:], T.hup[:].indirect(T.upg[:]), Fn.Identity, bias=1.5, scale=0.5))
+    wait("s", "act", a_up)
+    for k in range(4):
+        inc("dout", sc.dma_start(T.up[:, 256 * k:256 * k + 256], T.upr[32 * k:32 * k + 1, :]), 16)
+
+    wait("g", "sent", sent)
+    for name in ("vec", "act", "ten", "gpc", "dout"):
+        wait("g", name, cnt[name])

@@ -2,13 +2,16 @@ from concourse.bass import DstId, RemoteDMATransfer
 from concourse.mybir import dt, AluOpType as Op, ActivationFunctionType as Fn
 
 C, S, CAP, N = 1024, 256, 48, 8
-KEY = 2048
-NONE = N * KEY
-NEW = 1024
+ALL = N * CAP
+HALF = ALL // 2
 ZERO = 128
-NA, NB, B0 = 240, 144, 256
-ALL = B0 + NB
-PARTS = (("psa", 0, NA, 0, 16, 32), ("psb", B0, ALL, 32, 42, 52))
+LAND = ALL + ZERO
+MID = LAND // 2
+FAR = 1280
+UNIT = 1024
+SPARE = 64
+PAD = 4
+SEL = 24 + PAD
 
 E4, U8, F32, I32, U16, BF = "float8_e4m3fn_x4", "uint8", "float32", "int32", "uint16", "bfloat16"
 
@@ -19,72 +22,60 @@ def _sb(n, d):
 
 SCRATCH = {
     "grt": _sb(4 * S, BF), "gq": _sb(S, E4), "gs": _sb(S, U8),
-    "snw": _sb(24, I32), "soff": _sb(26, U16),
-    "slotq": _sb(336, E4), "slots": _sb(336, U8),
-    "landq": _sb(ZERO + ALL, E4), "lands": _sb(ZERO + ALL, U8),
-    "zt": _sb(512, BF), "eo": _sb(516, BF), "ef": _sb(516, BF), "en": _sb(516, BF),
+    "snw": _sb(24, I32), "soff": _sb(24, U16),
+    "slotq": _sb(ALL, E4), "slots": _sb(ALL, U8),
+    "landq": _sb(LAND, E4), "lands": _sb(LAND, U8),
+    "ef": _sb(516, BF), "en": _sb((C + SPARE) // 2, BF),
     "eq": _sb(1024, E4), "es": _sb(1024, U8),
     "wq": _sb(C, E4), "wqs": _sb(C, U8),
-    "finq": _sb(NEW + ZERO + ALL, E4), "fins": _sb(NEW + ZERO + ALL, U8),
+    "finq": _sb(C + ALL, E4), "fins": _sb(C + ALL, U8),
     "wselq": _sb(ALL, E4), "wsels": _sb(ALL, U8),
-    "firq": _sb(ALL, E4), "firs": _sb(ALL, U8),
-    "secq": _sb(ALL, E4), "secs": _sb(ALL, U8),
+    "parq": _sb(ALL, E4), "pars": _sb(ALL, U8),
     "h": _sb(4 * ALL, BF),
     "outq": _sb(C, E4), "outs": _sb(C, U8),
-    "tcw": _sb(24, I32), "ta": _sb(24, I32), "tb": _sb(24, I32), "tx": _sb(24, I32), "ty": _sb(24, I32),
-    "tz": _sb(24, I32),
-    "off4": _sb(32, U16), "wl": _sb(26, U16), "fsl": _sb(52, U16), "finl": _sb(64, U16), "upl": _sb(64, U16),
-    "upg": _sb(16, U16),
-    "pidx": _sb(2, I32), "pa": _sb(2, I32), "pcol": _sb(4, F32),
-    "m16": _sb(16, I32), "m16a": _sb(16, I32), "mk": _sb(ALL, F32), "seg": _sb(ALL, F32),
-    "vb": _sb(26, F32), "vw": _sb(26, F32), "cb": _sb(24, F32), "cl": _sb(24, F32),
-    "b48": _sb(48, F32), "vr": _sb(ALL, F32), "tab": _sb(C + CAP, F32), "pv": _sb(ALL, F32),
-    "sc1": _sb(ALL, F32), "sc2": _sb(ALL, F32), "fs": _sb(52, I32), "fa": _sb(52, I32),
-    "tw": _sb(64, F32), "ti": _sb(64, I32), "tf": _sb(64, I32),
-    "hup": _sb(16 + ALL, F32), "upr": _sb(256, F32),
+    "tcw": _sb(SEL + 16, I32), "ta": _sb(36, I32), "tb": _sb(36, I32), "tx": _sb(36, I32), "ty": _sb(36, I32),
+    "tz": _sb(36, I32), "off": _sb(36, U16), "wl": _sb(24, U16), "selo": _sb(2, U16),
+    "blk": _sb(128, F32), "blt": _sb(128, F32), "row": _sb(96, F32), "cb": _sb(36, F32), "cl": _sb(36, F32),
+    "vals": _sb(96, BF), "tab": _sb(C + SPARE, BF), "pv": _sb(LAND, BF),
+    "pt": _sb(ALL, BF), "t1": _sb(12, F32), "t2": _sb(12, F32), "zz": _sb(32, F32), "zt": _sb(32, F32),
+    "kk": _sb(32, F32), "dd": _sb(64, F32), "dr": _sb(64, F32), "pl": _sb(24, U16), "hy": _sb(32, BF),
+    "xx": _sb(64, BF), "xa": _sb(64, F32), "xb": _sb(64, F32), "xc": _sb(64, F32), "jw": _sb(64, F32),
+    "finl": _sb(64, U16), "upg": _sb(16, U16), "upr": _sb(256, F32),
     "psa": ("psum", [128, 2048], F32), "psb": ("psum", [128, 2048], F32),
 }
-SEMAPHORES = ["vec", "act", "ten", "gpc", "dsn", "dgr", "dtc", "dwc", "dws", "dfin", "dwrap", "dup", "dout",
+SEMAPHORES = ["vec", "act", "ten", "gpc", "dsn", "dgr", "dtc", "dwc", "dws", "dfin", "down", "dx", "dup", "dout",
               "arrec", "arres", "arrlc", "arrls", "sent", "issued"]
 
 
+def _rising(q):
+    return q >= N // 2
+
+
 def _stages(s):
-    return [(s + i) % N for i in range(1, 5)], [(s + i) % N for i in range(5, N)]
+    return ([q for q in range(N) if _rising(q) != _rising(s)],
+            [q for q in range(N) if _rising(q) == _rising(s) and q != s])
 
 
-def _chain(q):
-    return [(q - 4 + t) % N for t in range(N)]
-
-
-def _engines(s, stage, T, topo):
+def _engines(s, stage, T, topo, codes):
     src = T.cores[s]
-    have = len(topo.engines(src, T.cores[stage[0]]))
+    have = topo.engines(src, T.cores[stage[0]])
     size = 1
-    while 2 * size * len(stage) <= have:
+    while 2 * size * len(stage) <= len(have):
         size *= 2
-    spare = have - size * len(stage)
-    out, at = {}, 0
-    for q in stage:
+    spare = len(have) - size * len(stage)
+
+    def far(q):
         a, b = topo.chip(src), topo.chip(T.cores[q])
+        return not topo.mates(a, b) and not topo.same_plane(a, b)
+
+    order = sorted(stage, key=far, reverse=not codes)
+    out, at = {}, 0
+    for q in order:
         n = size
-        if spare >= size and not topo.mates(a, b) and not topo.same_plane(a, b):
+        if spare >= size and far(q):
             n, spare = 2 * size, spare - size
-        out[q] = topo.engines(src, T.cores[q])[at:at + n]
+        out[q] = have[at:at + n]
         at += n
-    return out
-
-
-def _pos(t):
-    return CAP * t if t < NA // CAP else CAP * t + B0 - NA
-
-
-def _runs(ranks):
-    out = []
-    for i, r in enumerate(ranks):
-        if out and out[-1][1] + out[-1][2] == r:
-            out[-1][2] += 1
-        else:
-            out.append([i, r, 1])
     return out
 
 
@@ -115,87 +106,69 @@ def rank_program(g, core, T, topo):
             seen[(qn, name)] = val
             {"v": ve, "s": sc, "t": te, "y": sy, "g": g}[qn].wait_ge(sem[name], val)
 
-    def iota(out, pattern, base):
-        return G(g.iota(out, pattern, base, 0, allow_small_or_imprecise_dtypes=True))
+    def iota(out, pattern, base, per=0):
+        return G(g.iota(out, pattern, base, per, allow_small_or_imprecise_dtypes=True))
 
-    one, two = _stages(me)
-    chain = _chain(me)
-    halves = ((0, chain[:5]), (16, chain[5:]))
     u8, u32 = dt.uint8, dt.uint32
+    up_ = _rising(me)
+    sign = 1 if up_ else -1
+    best = Op.max if up_ else Op.min
+    z0 = ZERO if up_ else 0
+    zz = 0 if up_ else ALL
+    t0 = 0 if up_ else PAD
+    p0 = 24 if up_ else 0
+    new0, old0 = (C, 0) if up_ else (0, ALL)
+    shift = FAR + UNIT
+    one, two = _stages(me)
+    early, late = (0, HALF) if up_ else (HALF, 0)
 
-    for k in range(8):
-        inc("dsn", (sc if k < 4 else sy).dma_start(T.snw[16 * k:16 * k + 16, :], T.sn[:]), 16)
     inc("dgr", sy.dma_start(T.grt[:], T.gr[:]), 16)
-    for k in range(8):
-        inc("dtc", (sc if k < 4 else sy).dma_start(T.tcw[16 * k:16 * k + 16, :], T.tc[:]), 16)
+    for k in range(4):
+        inc("dtc", sc.dma_start(T.tcw[16 * k:16 * k + 16, t0:t0 + 24], T.tc[:]), 16)
+    for k in range(4):
+        inc("dsn", sy.dma_start(T.snw[16 * k:16 * k + 16, :], T.sn[:]), 16)
     inc("dwc", sy.dma_start(T.wq[:].bitcast(u8), T.wc[:]), 16)
     inc("dws", sc.dma_start(T.wqs[:], T.ws[:]), 16)
 
-    v_eo = V(ve.memset(T.eo[:], 1.0))
-    v_zt = V(ve.memset(T.zt[:], 0.0))
-    p_tab = iota(T.tab[:, 0:64], [[16, 64]], NONE)
-    wait("g", "vec", v_eo)
-    p_ef = G(g.affine_select(T.ef[:], T.eo[:], [[1, 516]], Op.is_equal, 0.0, -3, -4))
-    p_m16 = G(g.iota(T.m16[:], [[1, 16]], 128, -1))
-    p_idx = G(g.iota(T.pidx[:], [[0, 2]], 0, 1))
-    p_cb = iota(T.cb[:], [[0, 8], [16, 3]], C)
-    p_b48 = iota(T.b48[:], [[1, 48]], 0)
-    for base, ranks in halves:
-        for i, r, n in _runs(ranks):
-            c = base + 3 * i
-            p_vb = iota(T.vb[:, c:c + 3 * n], [[KEY + CAP, n], [16, 3]], KEY * r + NEW + ZERO + 16 * c)
+    v_en = V(ve.memset(T.en[:], 0.0))
+    v_ef = V(ve.memset(T.ef[:], 0.0))
+    iota(T.blk[:, 0:32], [[48, 2], [48 * sign, 4], [16, 4]], 16 * t0, 3)
+    jw0 = old0 - new0 + z0 - MID
+    iota(T.blk[:, 64:96], [[0, 2], [1, 16]], jw0)
+    iota(T.blk[:, 32:64], [[48, 2], [0, 16]], z0 - MID - (0 if up_ else CAP), 3)
+    p_blk = iota(T.blk[:, 96:128], [[32, 32]], z0 - MID - sign * (6 * FAR + shift))
+    wait("g", "vec", v_ef)
+    diag = T.ef[:, 3:515:4]
+    p_ef = G(g.affine_select(diag, diag, [[1, 128]], Op.not_equal, 1.0, 0, -1))
+    p_cb = iota(T.cb[:], [[0, 9], [16, 4]], C - jw0)
+    p_row = iota(T.row[:], [[1, 96]], 0)
 
-    wait("s", "gpc", p_tab)
-    a_tab = 0
-    for r in (1, 2, 4, 8):
-        if a_tab:
-            wait("s", "act", a_tab)
-        a_tab = A(sc.activation(T.tab[:, 64 * r:128 * r], T.tab[:, 0:64 * r], Fn.Identity, bias=float(r)))
-    wait("s", "gpc", p_ef)
-    a_en = A(sc.activation(T.en[:], T.ef[:], Fn.Copy, scale=-0.125))
-    wait("s", "gpc", p_b48)
-    for t, s in enumerate(chain):
-        x = _pos(t)
-        a_vr = A(sc.activation(T.vr[:, x:x + CAP], T.b48[:], Fn.Identity, bias=float(KEY * s + NEW + ZERO + x)))
+    v_pad = V(ve.memset(T.tcw[:, p0:p0 + PAD], -1))
+    nobody = ZERO - 16 if up_ else ALL
+    v_pv = V(ve.memset(T.pv[:, nobody:nobody + 16], 0.0))
+    wait("v", "vec", v_en)
+    v_zq = V(ve.quantize_mx(T.landq[:, zz:zz + ZERO], T.lands[:, zz:zz + ZERO], T.en[:, 0:512]))
+    wait("v", "gpc", p_blk)
+    v_blt = V(ve.transpose(T.blt[:], T.blk[:]))
 
-    V(ve.memset(T.pv[:, 0:CAP], float(NONE)))
-    V(ve.memset(T.pv[:, NA:B0], float(NONE)))
-    V(ve.memset(T.tab[:, C:C + CAP], float(NONE)))
-    V(ve.memset(T.fs[:], 0))
-    v_vb = V(ve.memset(T.vb[:, 15:16], 0.0))
-    V(ve.memset(T.hup[:, 0:16], -3.0))
-    v_seg = V(ve.memset(T.seg[:], 1.0))
-    wait("v", "vec", v_zt)
-    v_zq = V(ve.quantize_mx(T.landq[:, 0:ZERO], T.lands[:, 0:ZERO], T.zt[:]))
-    wait("v", "vec", v_seg)
-    V(ve.memset(T.seg[:, 0:ALL:16], 0.0))
+    wait("s", "vec", v_en)
+    w = (C + SPARE) // 2
+    for i in range(2):
+        a_tab = A(sc.activation(T.tab[:, w * i:w * i + w], T.en[:], Fn.Identity, bias=float(-sign * FAR)))
+    wait("s", "vec", v_blt)
+    wait("s", "gpc", p_cb)
+    a_cl = A(sc.activation(T.cl[:], T.cb[:], Fn.Identity, bias=T.blt[:, 64:65]))
+    wait("s", "act", a_tab)
+    a_en = A(sc.activation(T.en[:, 3:515:4], diag, Fn.Copy, scale=-0.125))
+    wait("s", "gpc", p_row)
+    a_vals = A(sc.activation(T.vals[:], T.row[:], Fn.Identity, bias=T.blt[:, 32:33]))
+    a_kk = A(sc.activation(T.kk[:], T.row[:, 0:32], Fn.Identity, bias=T.blt[:, 96:97]))
+    a_jw = A(sc.activation(T.jw[:], T.row[:, 0:64], Fn.Identity, bias=T.blt[:, 64:65], scale=16.0))
 
     def unit(k, src):
         b = k % 4
         return V(ve.quantize_mx(T.eq[:, 128 * k:128 * k + 128], T.es[:, 128 * k:128 * k + 128],
                                 src[:, 3 - b:3 - b + 512]))
-
-    wait("v", "gpc", p_ef)
-    for k in range(4):
-        v_ep = unit(k, T.ef)
-    wait("v", "gpc", p_m16)
-    v = V(ve.tensor_scalar(T.m16a[:], T.m16[:], 15, None, Op.bitwise_and))
-    wait("v", "gpc", p_idx)
-    v_pa = V(ve.tensor_scalar(T.pa[:], T.pidx[:], 15, None, Op.bitwise_and))
-    wait("v", "vec", v)
-    v_mk = V(ve.tensor_scalar(T.mk[:, 0:16], T.m16a[:], 0.0, None, Op.is_equal))
-    wait("v", "vec", v_pa)
-    v_pc = V(ve.tensor_copy(T.pcol[:, 0:1], T.pa[:, 0:1]))
-
-    wait("v", "dsn", cnt["dsn"])
-    for base, ranks in ((0, one), (12, two), (22, [me])):
-        for i, r, n in _runs(ranks):
-            V(ve.tensor_copy(T.soff[:, base + 3 * i:base + 3 * (i + n)], T.snw[:, 3 * r:3 * (r + n)]))
-    wait("v", "gpc", p_cb)
-    wait("v", "vec", v_pc)
-    v_cl = V(ve.tensor_scalar(T.cl[:], T.cb[:], T.pcol[:, 0:1], None, Op.add))
-    wait("v", "dgr", cnt["dgr"])
-    v_gq = V(ve.quantize_mx(T.gq[:], T.gs[:], T.grt[:]))
 
     def pickc(out, a, b, win, w0, w1, off, o0, o1):
         return V(ve.tensor_copy(out[:, a:b].bitcast(u32), win[:, w0:w1].bitcast(u32).indirect(off[:, o0:o1])))
@@ -203,34 +176,60 @@ def rank_program(g, core, T, topo):
     def picks(out, a, b, win, w0, w1, off, o0, o1):
         return A(sc.activation(out[:, a:b], win[:, w0:w1].indirect(off[:, o0:o1]), Fn.Copy))
 
-    wait("v", "vec", v_gq)
-    wait("s", "vec", v_gq)
-    n1, n2 = CAP * len(one), CAP * (len(one) + len(two))
-    own = ZERO + _pos(chain.index(me))
-    v_p1 = pickc(T.slotq, 0, n1, T.gq, 0, S, T.soff, 0, 12)
-    a_p1 = picks(T.slots, 0, n1, T.gs, 0, S, T.soff, 0, 12)
+    wait("v", "vec", v_blt)
+    v = V(ve.tensor_scalar(T.selo[:, 0:1], T.blt[:, 0:1], 1.0 / 16, float(SEL - 1), Op.mult, Op.min))
     wait("v", "dtc", cnt["dtc"])
-    v_ta = V(ve.tensor_scalar(T.ta[:], T.tcw[:], 15, None, Op.bitwise_and))
-    v_p2 = pickc(T.slotq, n1, n2, T.gq, 0, S, T.soff, 12, 21)
-    a_p2 = picks(T.slots, n1, n2, T.gs, 0, S, T.soff, 12, 21)
-    V(ve.tensor_scalar(T.tb[:], T.tcw[:], 2047, 4, Op.bitwise_and, Op.logical_shift_right))
-    wait("v", "vec", v_ta)
-    v_tx = V(ve.tensor_scalar(T.tx[:], T.ta[:], 64.0, None, Op.mult))
-    v_own = pickc(T.landq, own, own + CAP, T.gq, 0, S, T.soff, 22, 25)
-    a_own = picks(T.lands, own, own + CAP, T.gs, 0, S, T.soff, 22, 25)
-    wait("v", "vec", v_tx)
-    v_ty = V(ve.tensor_tensor(T.ty[:], T.tx[:], T.tb[:], Op.add))
+    lo, hi = slice(0, 64), slice(64, 128)
+    v = V(ve.tensor_copy(T.tcw[hi, t0:t0 + 24], T.tcw[lo, t0:t0 + 24]))
+    v_zz = V(ve.memset(T.zz[:, 12:32], 0.0))
+    wait("v", "vec", v)
+    v = V(ve.tensor_copy(T.tcw[:, SEL:SEL + 16], T.tcw[:, 0:SEL].indirect(T.selo[:, 0:1])))
+    v_wl = V(ve.tensor_copy(T.wl[:], T.tcw[:, t0:t0 + 24]))
+    wait("v", "gpc", p_ef)
+    unit(0, T.ef)
+    wait("v", "vec", v)
+    v = V(ve.tensor_scalar(T.ta[:], T.tcw[:, 0:36], 15, None, Op.bitwise_and))
+    V(ve.tensor_scalar(T.tb[:], T.tcw[:, 0:36], 2047, 4, Op.bitwise_and, Op.logical_shift_right))
+    wait("v", "vec", v)
+    v = V(ve.tensor_scalar(T.tx[:], T.ta[:], 64.0, None, Op.mult))
+    unit(1, T.ef)
+    wait("v", "vec", v)
+    v = V(ve.tensor_tensor(T.ty[:], T.tx[:], T.tb[:], Op.add))
+    unit(2, T.ef)
+    wait("v", "vec", v)
+    wait("v", "act", a_cl)
+    v = V(ve.tensor_tensor(T.tz[:], T.ty[:], T.cl[:], Op.min))
+
+    wait("v", "dgr", cnt["dgr"])
+    v_gq = V(ve.quantize_mx(T.gq[:], T.gs[:], T.grt[:]))
+    wait("v", "dsn", cnt["dsn"])
+    V(ve.tensor_copy(T.soff[lo, :], T.snw[lo, :]))
+    v_so = V(ve.tensor_copy(T.soff[hi, :], T.snw[lo, :]))
+    wait("v", "vec", v)
+    v_off = V(ve.tensor_copy(T.off[:], T.tz[:]))
+    wait("v", "vec", v_so)
+    wait("s", "vec", v_so)
+    v_p1 = pickc(T.slotq, early, early + HALF, T.gq, 0, S, T.soff, early // 16, early // 16 + 12)
+    a_p1 = picks(T.slots, early, early + HALF, T.gs, 0, S, T.soff, early // 16, early // 16 + 12)
+    own, nxt = (0, CAP) if up_ else (CAP, 0)
+    wait("v", "vec", v_off)
+    wait("v", "act", a_vals)
+    v_s1 = V(ve.tensor_copy(T.tab[:].indirect(T.off[:, SEL:SEL + 3]), T.vals[:, own:own + CAP]))
+    v_p2 = pickc(T.slotq, late, late + HALF, T.gq, 0, S, T.soff, late // 16, late // 16 + 12)
+    wait("s", "vec", v_s1)
+    a_pv = A(sc.activation(T.pv[:, z0:z0 + ALL], T.tab[:].indirect(T.off[:, t0:t0 + 24]), Fn.Copy))
+    a_p2 = picks(T.slots, late, late + HALF, T.gs, 0, S, T.soff, late // 16, late // 16 + 12)
 
     sent = 0
-    for stage, a, vp, ap, cs, ss in ((one, 0, v_p1, a_p1, "arrec", "arres"), (two, n1, v_p2, a_p2, "arrlc", "arrls")):
-        eng = _engines(me, stage, T, topo)
+    for stage, vp, ap, cs, ss in ((one, v_p1, a_p1, "arrec", "arres"), (two, v_p2, a_p2, "arrlc", "arrls")):
         for codes in (True, False):
+            eng = _engines(me, stage, T, topo, codes)
             wait("g", "vec" if codes else "act", vp if codes else ap)
             tr = []
-            for i, q in enumerate(stage):
+            for q in stage:
                 rid, pid, _se = topo.addr(T.cores[q])
-                x = a + CAP * i
-                y = ZERO + _pos(_chain(q).index(me))
+                x = CAP * q
+                y = (ZERO if _rising(q) else 0) + CAP * me
                 src, dst = ((T.slotq[:, x:x + CAP].bitcast(u8), T.landq[:, y:y + CAP].bitcast(u8)) if codes
                             else (T.slots[:, x:x + CAP], T.lands[:, y:y + CAP]))
                 tr.append(RemoteDMATransfer(dst_ids=[DstId(rid=rid, pnc=pid)],
@@ -240,193 +239,159 @@ def rank_program(g, core, T, topo):
             g.remote_dma_fused(tr, local_sem=sem["sent"])
     g.sem_inc(sem["issued"], 1)
 
-    wait("y", "issued", 1)
-    inc("dfin", sy.dma_start(T.finq[:, 0:C // 2].bitcast(u8), T.wc[:, 0:2 * C]), 16)
+    def prod(ps, b, k, q, s, a, start, stop):
+        return te.matmul_mx(T[ps][:, 512 * b:512 * b + HALF], T.eq[:, 128 * k:128 * k + 128],
+                            T.es[:, 128 * k:128 * k + 128], T[q][:, a:a + HALF], T[s][:, a:a + HALF], start, stop)
 
-    wait("s", "vec", v_mk)
-    a_mk, n = 0, 16
-    while n < ALL:
-        m = min(n, ALL - n)
-        if a_mk:
-            wait("s", "act", a_mk)
-        a_mk = A(sc.activation(T.mk[:, n:n + m], T.mk[:, 0:m], Fn.Copy))
-        n += m
-    wait("s", "gpc", p_vb)
-    wait("s", "vec", max(v_pc, v_vb))
-    a_vw = A(sc.activation(T.vw[:, 0:25], T.vb[:, 0:25], Fn.Identity, bias=T.pcol[:, 0:1]))
+    parts = (("psa", early), ("psb", late))
 
-    late, todo = {}, []
-
-    def do_wl(a, b, x, y):
-        late["wl"] = V(ve.tensor_copy(T.wl[:, a:b], T.tcw[:, x:y]))
-
-    def do_em(k):
-        wait("v", "act", a_en)
-        late["em"] = unit(k, T.en)
-
-    def do_w(a, b):
+    def table_columns(ps, a):
         wait("v", "dwc", cnt["dwc"])
-        wait("v", "vec", late["wl"])
         wait("s", "dws", cnt["dws"])
-        wait("s", "vec", late["wl"])
-        late["w"] = pickc(T.wselq, a, b, T.wq, 0, C, T.wl, a // 16, b // 16)
-        late["ws"] = picks(T.wsels, a, b, T.wqs, 0, C, T.wl, a // 16, b // 16)
-
-    def do_list(part, step):
-        _ps, a, z, x, y, e = part
-        key, n = ("list", a), (z - a) // 16
-        if step == 0:
-            wait("v", "act", a_mk)
-            wait("v", "vec", late["pv"])
-            late[key] = V(ve.tensor_tensor_scan(T.sc1[:, a:z], T.pv[:, a:z], T.mk[:, a:z], 0.0, Op.add, Op.mult))
-            return
-        wait("v", "vec", late[key])
-        if step == 1:
-            late[key] = V(ve.tensor_tensor_scan(T.sc2[:, a:z], T.seg[:, a:z], T.sc1[:, a:z], 0.0, Op.mult, Op.add))
-        elif step == 2:
-            wait("v", "act", a_vw)
-            gw, mine = T.sc2[:, a + 15:z:16], T.vw[:, a // 16:z // 16]
-            V(ve.tensor_tensor(T.fs[:, x:x + n], mine, gw, Op.min))
-            late[key] = V(ve.tensor_tensor(T.fs[:, y:y + n], mine, gw, Op.max))
-        elif step == 3:
-            late[key] = V(ve.tensor_scalar(T.fa[:, x:e], T.fs[:, x:e], KEY - 1, None, Op.bitwise_and))
-        else:
-            late[key] = V(ve.tensor_scalar(T.fsl[:, x:e], T.fa[:, x:e], float(NEW), float(NEW), Op.max, Op.subtract))
-
-    for base, ranks in halves:
-        for i, r, n in _runs(ranks):
-            todo.append((do_wl, (base + 3 * i, base + 3 * (i + n), 3 * r, 3 * (r + n))))
-    for k in range(4, 8):
-        todo.append((do_em, (k,)))
-    todo.append((do_w, (0, NA)))
-    todo.append((do_w, (B0, ALL)))
-
-    def filler(n=1):
-        for _i in range(n):
-            if todo:
-                f, args = todo.pop(0)
-                f(*args)
-
-    filler()
-    wait("v", "vec", max(v_ty, v_cl))
-    v_tz = V(ve.tensor_tensor(T.tz[:], T.ty[:], T.cl[:], Op.min))
-    filler()
-    wait("v", "vec", v_tz)
-    for i in range(3):
-        v_off = V(ve.tensor_copy(T.off4[:, i:32:4], T.tz[:, i:24:3]))
-    filler()
-    wait("v", "act", max(a_tab, a_vr))
-    wait("v", "vec", v_off)
-    v_sc = 0
-    for t, s in enumerate(chain):
-        x = _pos(t)
-        win = T.tab[:, 0:C + CAP]
-        off = T.off4[:, 4 * s:4 * s + 3]
-        if t:
-            wait("v", "vec", v_sc)
-            late["pv"] = V(ve.tensor_copy(T.pv[:, x:x + CAP], win.indirect(off)))
-            if t == 4:
-                filler(len(todo))
-                todo.extend((do_list, (PARTS[0], k)) for k in range(5))
-            else:
-                filler()
-            wait("v", "vec", late["pv"])
-        v_sc = V(ve.tensor_copy(win.indirect(off), T.vr[:, x:x + CAP]))
-        if t:
-            filler()
-    filler(len(todo))
-    wait("y", "vec", v_sc)
-    for k in range(8):
-        inc("dwrap", sy.dma_start(T.tw[16 * k:16 * k + 16, :], T.tab[16 * k:16 * k + 1, 0:C]), 16)
-    inc("dfin", sy.dma_start(T.finq[:, C // 2:C].bitcast(u8), T.wc[:, 2 * C:4 * C]), 16)
-    inc("dfin", sy.dma_start(T.fins[:, 0:C], T.ws[:]), 16)
-    for k in range(5):
-        do_list(PARTS[1], k)
-    wait("s", "vec", late["pv"])
-    a_h = A(sc.activation(T.hup[:, 16:16 + ALL], T.pv[:], Fn.Sign, bias=float(NONE - KEY // 8), scale=-1.0))
-
-    def prod(ps, b, k, q, s, a, z, start, stop):
-        return te.matmul_mx(T[ps][:, 512 * b:512 * b + z - a], T.eq[:, 128 * k:128 * k + 128],
-                            T.es[:, 128 * k:128 * k + 128], T[q][:, a:z], T[s][:, a:z], start, stop)
-
-    wait("t", "vec", max(late["w"], v_ep))
-    wait("t", "act", late["ws"])
-    for ps, a, z, _x, _y, _e in PARTS:
+        wait("t", "vec", pickc(T.wselq, a, a + HALF, T.wq, 0, C, T.wl, a // 16, a // 16 + 12))
+        wait("t", "act", picks(T.wsels, a, a + HALF, T.wqs, 0, C, T.wl, a // 16, a // 16 + 12))
         for b in range(4):
-            prod(ps, b, b, "wselq", "wsels", a, z, True, False)
+            prod(ps, b, b, "wselq", "wsels", a, True, False)
 
-    def arrived(stage):
-        return sum(len(_engines(s, _stages(s)[stage], T, topo)[me])
+    q0, q1 = slice(0, 32), slice(32, 64)
+    quads = [slice(32 * k, 32 * k + 32) for k in range(4)]
+    unit(3, T.ef)
+    wait("v", "act", a_pv)
+    v = V(ve.transpose(T.pt[:], T.pv[:, z0:z0 + ALL]))
+    v_s2 = V(ve.tensor_copy(T.tab[:].indirect(T.off[:, SEL + 4:SEL + 7]), T.vals[:, nxt:nxt + CAP]))
+    wait("v", "vec", v)
+    v = V(ve.tensor_tensor(T.t1[:], T.pt[:, 0:ALL:32], T.pt[:, 16:ALL:32], Op.add))
+    unit(4, T.en)
+    wait("v", "vec", v)
+    v = V(ve.tensor_tensor(T.t2[lo, :], T.t1[lo, :], T.t1[hi, :], Op.add))
+    wait("v", "vec", v)
+    v = V(ve.tensor_tensor(T.zz[q0, 0:12], T.t2[q0, :], T.t2[q1, :], Op.add))
+    wait("v", "vec", v)
+    for qk in quads[1:]:
+        v = V(ve.tensor_copy(T.zz[qk, 0:12], T.zz[q0, 0:12]))
+    unit(5, T.en)
+    wait("v", "vec", v)
+    v = V(ve.transpose(T.zt[:], T.zz[:]))
+    table_columns(*parts[0])
+    wait("v", "vec", v)
+    wait("v", "act", a_jw)
+    for x, y, n in ((16, 0, 32), (0, 0, 16), (48, 16, 16)):
+        v = V(ve.tensor_tensor(T.dd[:, x:x + n], T.zt[:, y:y + n], T.kk[:, y:y + n], Op.subtract))
+    wait("v", "vec", v)
+    v = V(ve.transpose(T.dr[:], T.dd[:]))
+    v_hy = V(ve.tensor_scalar(T.hy[:], T.dd[:, 16:48], sign / UNIT, 2.0, Op.mult, Op.min))
+    unit(6, T.en)
+    wait("v", "vec", v)
+    wins = ((0, ZERO + HALF) if up_ else (HALF, LAND), (0, LAND))
+    v_pl = []
+    for (ps, a), (w0, w1) in zip(parts, wins):
+        top = w1 - 1 if up_ else ALL - w0
+        for e in range(2):
+            c = 32 * e + a // 32
+            v = V(ve.tensor_scalar(T.pl[:, a // 16 + e:a // 16 + 12:2], T.dr[:, c:c + 6],
+                                   float(MID - sign * shift - w0), float(top), Op.add, Op.min))
+        v_pl.append(v)
+    v_em = unit(7, T.en)
+    table_columns(*parts[1])
+
+    x = CAP * me
+    wait("y", "vec", v_p2)
+    wait("y", "act", a_p2)
+    inc("down", sy.dma_start(T.landq[:, z0 + x:z0 + x + CAP].bitcast(u8), T.slotq[:, x:x + CAP].bitcast(u8)), 16)
+    inc("down", sy.dma_start(T.lands[:, z0 + x:z0 + x + CAP], T.slots[:, x:x + CAP]), 16)
+    wait("y", "vec", v_s2)
+    for i, qk in enumerate(quads):
+        k = 32 * i + (0 if up_ else 16)
+        inc("dx", sy.dma_start(T.xx[qk, :], T.tab[k:k + 2, 0:C]), 16)
+    wait("y", "issued", 1)
+    inc("dfin", sy.dma_start(T.finq[:, old0:old0 + C // 2].bitcast(u8), T.wc[:, 0:2 * C]), 16)
+    wait("y", "vec", v_hy)
+    for k in range(4):
+        inc("dup", sy.dma_start(T.pv[32 * k:32 * k + 1, z0:z0 + ALL], T.hy[32 * k:32 * k + 12, :]), 16)
+    inc("dfin", sy.dma_start(T.finq[:, old0 + C // 2:old0 + C].bitcast(u8), T.wc[:, 2 * C:4 * C]), 16)
+    inc("dfin", sy.dma_start(T.fins[:, old0:old0 + C], T.ws[:]), 16)
+
+    def arrived(stage, codes):
+        return sum(len(_engines(s, _stages(s)[stage], T, topo, codes)[me])
                    for s in range(N) if s != me and me in _stages(s)[stage])
 
     stops = []
-    for i, (ps, a, z, x, y, e) in enumerate(PARTS):
-        w1, n = ZERO + z, (z - a) // 16
-        wait("v", "arrec" if i == 0 else "arrlc", arrived(i))
-        wait("s", "arres" if i == 0 else "arrls", arrived(i))
-        wait("v", "vec", max(late["list", a], v_own, v_zq))
-        wait("s", "vec", max(late["list", a], v_zq))
-        wait("s", "act", a_own)
-        for q, s, o, last in (("firq", "firs", x, False), ("secq", "secs", y, True)):
-            vp = pickc(T[q], a, z, T.landq, 0, w1, T.fsl, o, o + n)
-            ap = picks(T[s], a, z, T.lands, 0, w1, T.fsl, o, o + n)
-            wait("t", "vec", max(vp, late["em"]))
-            wait("t", "act", ap)
+
+    def part(i):
+        (ps, a), (w0, w1) = parts[i], wins[i]
+        cs, ss = ("arrec", "arres") if i == 0 else ("arrlc", "arrls")
+        for qn in "vt":
+            wait(qn, cs, arrived(i, True))
+        for qn in "st":
+            wait(qn, ss, arrived(i, False))
+        if i:
+            for qn in "vst":
+                wait(qn, "down", cnt["down"])
+        wait("v", "vec", v_pl[i])
+        wait("s", "vec", v_pl[i])
+        vp = pickc(T.parq, a, a + HALF, T.landq, w0, w1, T.pl, a // 16, a // 16 + 12)
+        ap = picks(T.pars, a, a + HALF, T.lands, w0, w1, T.pl, a // 16, a // 16 + 12)
+        wait("t", "vec", v_em)
+        if not up_:
             for b in range(4):
-                ins = prod(ps, b, 4 + b, q, s, a, z, False, last)
-                if last:
-                    stops.append(inc("ten", ins))
+                prod(ps, b, 4 + b, "landq", "lands", z0 + a, False, False)
+        wait("t", "vec", vp)
+        wait("t", "act", ap)
+        for b in range(4):
+            ins = prod(ps, b, 4 + b, "parq", "pars", a, False, not up_)
+            if up_:
+                ins = prod(ps, b, 4 + b, "landq", "lands", z0 + a, False, True)
+            stops.append(inc("ten", ins))
 
-    wait("v", "dwrap", cnt["dwrap"])
-    v_ti = V(ve.tensor_copy(T.ti[:], T.tw[:]))
+    part(0)
+    wait("v", "dx", cnt["dx"])
+    v = V(ve.tensor_tensor(T.xa[lo, :], T.xx[lo, :], T.xx[hi, :], best))
+    wait("v", "vec", v)
+    v = V(ve.tensor_tensor(T.xb[q0, :], T.xa[q0, :], T.xa[q1, :], best))
+    wait("v", "vec", v)
+    v = V(ve.tensor_tensor(T.xc[q0, :], T.xb[q0, :], T.jw[q0, :], best))
+    wait("v", "vec", v)
+    u0, u1 = (nobody, LAND) if up_ else (0, nobody + 16)
+    for k, qk in enumerate(quads):
+        v_up = V(ve.tensor_scalar(T.upg[qk, :], T.xc[q0, 16 * k:16 * k + 16],
+                                  float((ZERO - 1 if up_ else ALL) - MID), float(MID - u0), best, Op.add))
+    part(1)
+    for qk in quads:
+        V(ve.tensor_scalar(T.finl[qk, :], T.xc[q0, :], float(new0 - z0 + MID), None, Op.add))
 
-    for i, (ps, a, z, _x, _y, _e) in enumerate(PARTS):
+    for i, (ps, a) in enumerate(parts):
         vl = al = 0
         for b in range(4):
-            out, src = T.h[:, 4 * a + b:4 * z:4], T[ps][:, 512 * b:512 * b + z - a]
-            if b % 2 == 0:
+            out, src = T.h[:, 4 * a + b:4 * (a + HALF):4], T[ps][:, 512 * b:512 * b + HALF]
+            if b % 2:
                 wait("v", "ten", stops[4 * i + b])
                 vl = V(ve.tensor_copy(out, src))
-                if i == 0 and b == 0:
-                    wait("v", "vec", v_ti)
-                    v_tf = V(ve.tensor_scalar(T.tf[:], T.ti[:], KEY - 1, None, Op.bitwise_and))
             else:
                 wait("s", "ten", stops[4 * i + b])
                 al = A(sc.activation(out, src, Fn.Copy))
-        if i == 0:
-            wait("v", "vec", v_tf)
-            v_up = V(ve.tensor_scalar(T.upl[:], T.tf[:], float(NEW + ZERO - 16), float(NEW + ZERO - 16),
-                                      Op.max, Op.subtract))
-            v_fin = V(ve.tensor_copy(T.finl[:], T.tf[:]))
         wait("v", "vec", vl)
         wait("v", "act", al)
-        x = NEW + ZERO
-        v_q = V(ve.quantize_mx(T.finq[:, x + a:x + z], T.fins[:, x + a:x + z], T.h[:, 4 * a:4 * z]))
+        x = new0 + a
+        v_q = V(ve.quantize_mx(T.finq[:, x:x + HALF], T.fins[:, x:x + HALF], T.h[:, 4 * a:4 * (a + HALF)]))
+        if i == 0:
+            wait("s", "dup", cnt["dup"])
+            wait("s", "vec", v_up)
+            a_up = A(sc.activation(T.upr[:], T.pv[:, u0:u1].indirect(T.upg[:]), Fn.Relu))
+            wait("y", "act", a_up)
+            inc("dout", sy.dma_start(T.up[:], T.upr[0:128:32, :]), 16)
 
-    wait("y", "vec", v_up)
-    for k in range(8):
-        c = 16 * (k // 2)
-        inc("dup", sy.dma_start(T.upg[16 * k:16 * k + 16, :], T.upl[16 * k:16 * k + 16, c:c + 16]), 16)
-
-    wait("v", "vec", max(v_q, v_fin))
+    wait("v", "vec", v_q)
     wait("v", "dfin", cnt["dfin"])
-    wait("s", "vec", max(v_q, v_fin))
+    wait("s", "vec", v_q)
     wait("s", "dfin", cnt["dfin"])
-    W = NEW + ZERO + ALL
     for j in range(4):
-        vp = pickc(T.outq, 256 * j, 256 * j + 256, T.finq, 0, W, T.finl, 16 * j, 16 * j + 16)
-        ap = picks(T.outs, 256 * j, 256 * j + 256, T.fins, 0, W, T.finl, 16 * j, 16 * j + 16)
+        vp = pickc(T.outq, 256 * j, 256 * j + 256, T.finq, 0, C + ALL, T.finl, 16 * j, 16 * j + 16)
+        ap = picks(T.outs, 256 * j, 256 * j + 256, T.fins, 0, C + ALL, T.finl, 16 * j, 16 * j + 16)
         wait("y", "vec", vp)
         inc("dout", sy.dma_start(T.oc[:, 1024 * j:1024 * j + 1024], T.outq[:, 256 * j:256 * j + 256].bitcast(u8)), 16)
-    wait("y", "act", ap)
+    wait("s", "act", ap)
     for k in range(4):
-        inc("dout", sy.dma_start(T.osc[4 * k:4 * k + 4, :], T.outs[32 * k:32 * k + 4, :]), 16)
-    wait("s", "dup", cnt["dup"])
-    wait("s", "act", a_h)
-    a_up = A(sc.activation(T.upr[:], T.hup[:].indirect(T.upg[:]), Fn.Identity, bias=1.5, scale=0.5))
-    wait("s", "act", a_up)
-    for k in range(4):
-        inc("dout", sc.dma_start(T.up[:, 256 * k:256 * k + 256], T.upr[32 * k:32 * k + 1, :]), 16)
+        inc("dout", sc.dma_start(T.osc[4 * k:4 * k + 4, :], T.outs[32 * k:32 * k + 4, :]), 16)
 
     wait("g", "sent", sent)
     for name in ("vec", "act", "ten", "gpc", "dout"):

@@ -4,14 +4,10 @@ from concourse.mybir import dt, AluOpType as Op, ActivationFunctionType as Fn
 C, S, CAP, N = 1024, 256, 48, 8
 ALL = N * CAP
 HALF = ALL // 2
-ZERO = 128
-LAND = ALL + ZERO
+LAND = ALL + 128
 MID = LAND // 2
 FAR = 1280
-UNIT = 1024
-SPARE = 64
-PAD = 4
-SEL = 24 + PAD
+PIECES = (256, 256, 256, 160, 96)
 
 E4, U8, F32, I32, U16, BF = "float8_e4m3fn_x4", "uint8", "float32", "int32", "uint16", "bfloat16"
 
@@ -25,39 +21,39 @@ SCRATCH = {
     "snw": _sb(24, I32), "soff": _sb(24, U16),
     "slotq": _sb(ALL, E4), "slots": _sb(ALL, U8),
     "landq": _sb(LAND, E4), "lands": _sb(LAND, U8),
-    "ef": _sb(516, BF), "en": _sb((C + SPARE) // 2, BF),
+    "ef": _sb(516, BF), "en": _sb(516, BF),
     "eq": _sb(1024, E4), "es": _sb(1024, U8),
     "wq": _sb(C, E4), "wqs": _sb(C, U8),
-    "finq": _sb(C + ALL, E4), "fins": _sb(C + ALL, U8),
+    "finq": _sb(ALL + C, E4), "fins": _sb(ALL + C, U8),
     "wselq": _sb(ALL, E4), "wsels": _sb(ALL, U8),
     "parq": _sb(ALL, E4), "pars": _sb(ALL, U8),
     "h": _sb(4 * ALL, BF),
     "outq": _sb(C, E4), "outs": _sb(C, U8),
-    "tcw": _sb(SEL + 16, I32), "ta": _sb(36, I32), "tb": _sb(36, I32), "tx": _sb(36, I32), "ty": _sb(36, I32),
-    "tz": _sb(36, I32), "off": _sb(36, U16), "wl": _sb(24, U16), "selo": _sb(2, U16),
-    "blk": _sb(128, F32), "blt": _sb(128, F32), "row": _sb(96, F32), "cb": _sb(36, F32), "cl": _sb(36, F32),
-    "vals": _sb(96, BF), "tab": _sb(C + SPARE, BF), "pv": _sb(LAND, BF),
+    "tcw": _sb(24, I32), "tu": _sb(24, I32), "mine": _sb(16, I32), "tz": _sb(4, I32), "cl": _sb(4, I32),
+    "off": _sb(4, U16), "wl": _sb(24, U16), "selo": _sb(4, U16),
+    "blk": _sb(96, F32), "blt": _sb(96, F32), "kc": _sb(2, F32), "pc": _sb(4, F32), "pd": _sb(4, F32),
+    "vals": _sb(CAP, BF), "tab": _sb(C + ALL + 16, BF), "pv": _sb(ALL + 16, BF),
     "pt": _sb(ALL, BF), "t1": _sb(12, F32), "t2": _sb(12, F32), "zz": _sb(32, F32), "zt": _sb(32, F32),
-    "kk": _sb(32, F32), "dd": _sb(64, F32), "dr": _sb(64, F32), "pl": _sb(24, U16), "hy": _sb(32, BF),
-    "xx": _sb(64, BF), "xa": _sb(64, F32), "xb": _sb(64, F32), "xc": _sb(64, F32), "jw": _sb(64, F32),
-    "finl": _sb(64, U16), "upg": _sb(16, U16), "upr": _sb(256, F32),
+    "dd": _sb(64, F32), "dr": _sb(64, F32), "pl": _sb(24, U16), "hy": _sb(32, BF),
+    "tt": _sb(C, BF), "x1": _sb(32, F32), "x2": _sb(32, F32), "x3": _sb(32, F32), "xt": _sb(32, F32),
+    "jw": _sb(32, F32), "xe": _sb(32, F32), "xd": _sb(64, F32), "xr": _sb(64, F32), "finl": _sb(64, U16),
+    "upg": _sb(16, U16), "upr": _sb(256, F32),
     "psa": ("psum", [128, 2048], F32), "psb": ("psum", [128, 2048], F32),
 }
-SEMAPHORES = ["vec", "act", "ten", "gpc", "dsn", "dgr", "dtc", "dwc", "dws", "dfin", "down", "dx", "dup", "dout",
+SEMAPHORES = ["vec", "act", "ten", "gpc", "dsn", "dgr", "dgs", "dtc", "dwc", "dws", "dfin", "down", "dup", "dout",
               "arrec", "arres", "arrlc", "arrls", "sent", "issued"]
 
 
-def _rising(q):
+def _upper(q):
     return q >= N // 2
 
 
 def _stages(s):
-    return ([q for q in range(N) if _rising(q) != _rising(s)],
-            [q for q in range(N) if _rising(q) == _rising(s) and q != s])
+    return ([q for q in range(N) if _upper(q) != _upper(s)],
+            [q for q in range(N) if _upper(q) == _upper(s) and q != s])
 
 
-def _engines(s, stage, T, topo, codes):
-    src = T.cores[s]
+def _engines(src, stage, T, topo, codes):
     have = topo.engines(src, T.cores[stage[0]])
     size = 1
     while 2 * size * len(stage) <= len(have):
@@ -68,15 +64,27 @@ def _engines(s, stage, T, topo, codes):
         a, b = topo.chip(src), topo.chip(T.cores[q])
         return not topo.mates(a, b) and not topo.same_plane(a, b)
 
-    order = sorted(stage, key=far, reverse=not codes)
     out, at = {}, 0
-    for q in order:
+    for q in sorted(stage, key=far, reverse=not codes):
         n = size
         if spare >= size and far(q):
             n, spare = 2 * size, spare - size
         out[q] = have[at:at + n]
         at += n
     return out
+
+
+def _spread(g, core, s, stage, codes, name, T, topo):
+    eng, tr = _engines(core, stage, T, topo, codes), []
+    for q in stage:
+        rid, pid, _se = topo.addr(T.cores[q])
+        x, y = CAP * q, CAP * s
+        src, dst = ((T.slotq[:, x:x + CAP].bitcast(dt.uint8), T.landq[:, y:y + CAP].bitcast(dt.uint8)) if codes
+                    else (T.slots[:, x:x + CAP], T.lands[:, y:y + CAP]))
+        tr.append(RemoteDMATransfer(dst_ids=[DstId(rid=rid, pnc=pid)], dma_engine_mask=sum(1 << e for e in eng[q]),
+                                    remote_sem=T.sem[name], src=src, dst=dst))
+    g.remote_dma_fused(tr, local_sem=T.sem["sent"])
+    return sum(len(e) for e in eng.values())
 
 
 def rank_program(g, core, T, topo):
@@ -106,64 +114,11 @@ def rank_program(g, core, T, topo):
             seen[(qn, name)] = val
             {"v": ve, "s": sc, "t": te, "y": sy, "g": g}[qn].wait_ge(sem[name], val)
 
+    def after(v):
+        wait("v", "vec", v)
+
     def iota(out, pattern, base, per=0):
         return G(g.iota(out, pattern, base, per, allow_small_or_imprecise_dtypes=True))
-
-    u8, u32 = dt.uint8, dt.uint32
-    up_ = _rising(me)
-    sign = 1 if up_ else -1
-    best = Op.max if up_ else Op.min
-    z0 = ZERO if up_ else 0
-    zz = 0 if up_ else ALL
-    t0 = 0 if up_ else PAD
-    p0 = 24 if up_ else 0
-    new0, old0 = (C, 0) if up_ else (0, ALL)
-    shift = FAR + UNIT
-    one, two = _stages(me)
-    early, late = (0, HALF) if up_ else (HALF, 0)
-
-    inc("dgr", sy.dma_start(T.grt[:], T.gr[:]), 16)
-    for k in range(4):
-        inc("dtc", sc.dma_start(T.tcw[16 * k:16 * k + 16, t0:t0 + 24], T.tc[:]), 16)
-    for k in range(4):
-        inc("dsn", sy.dma_start(T.snw[16 * k:16 * k + 16, :], T.sn[:]), 16)
-    inc("dwc", sy.dma_start(T.wq[:].bitcast(u8), T.wc[:]), 16)
-    inc("dws", sc.dma_start(T.wqs[:], T.ws[:]), 16)
-
-    v_en = V(ve.memset(T.en[:], 0.0))
-    v_ef = V(ve.memset(T.ef[:], 0.0))
-    iota(T.blk[:, 0:32], [[48, 2], [48 * sign, 4], [16, 4]], 16 * t0, 3)
-    jw0 = old0 - new0 + z0 - MID
-    iota(T.blk[:, 64:96], [[0, 2], [1, 16]], jw0)
-    iota(T.blk[:, 32:64], [[48, 2], [0, 16]], z0 - MID - (0 if up_ else CAP), 3)
-    p_blk = iota(T.blk[:, 96:128], [[32, 32]], z0 - MID - sign * (6 * FAR + shift))
-    wait("g", "vec", v_ef)
-    diag = T.ef[:, 3:515:4]
-    p_ef = G(g.affine_select(diag, diag, [[1, 128]], Op.not_equal, 1.0, 0, -1))
-    p_cb = iota(T.cb[:], [[0, 9], [16, 4]], C - jw0)
-    p_row = iota(T.row[:], [[1, 96]], 0)
-
-    v_pad = V(ve.memset(T.tcw[:, p0:p0 + PAD], -1))
-    nobody = ZERO - 16 if up_ else ALL
-    v_pv = V(ve.memset(T.pv[:, nobody:nobody + 16], 0.0))
-    wait("v", "vec", v_en)
-    v_zq = V(ve.quantize_mx(T.landq[:, zz:zz + ZERO], T.lands[:, zz:zz + ZERO], T.en[:, 0:512]))
-    wait("v", "gpc", p_blk)
-    v_blt = V(ve.transpose(T.blt[:], T.blk[:]))
-
-    wait("s", "vec", v_en)
-    w = (C + SPARE) // 2
-    for i in range(2):
-        a_tab = A(sc.activation(T.tab[:, w * i:w * i + w], T.en[:], Fn.Identity, bias=float(-sign * FAR)))
-    wait("s", "vec", v_blt)
-    wait("s", "gpc", p_cb)
-    a_cl = A(sc.activation(T.cl[:], T.cb[:], Fn.Identity, bias=T.blt[:, 64:65]))
-    wait("s", "act", a_tab)
-    a_en = A(sc.activation(T.en[:, 3:515:4], diag, Fn.Copy, scale=-0.125))
-    wait("s", "gpc", p_row)
-    a_vals = A(sc.activation(T.vals[:], T.row[:], Fn.Identity, bias=T.blt[:, 32:33]))
-    a_kk = A(sc.activation(T.kk[:], T.row[:, 0:32], Fn.Identity, bias=T.blt[:, 96:97]))
-    a_jw = A(sc.activation(T.jw[:], T.row[:, 0:64], Fn.Identity, bias=T.blt[:, 64:65], scale=16.0))
 
     def unit(k, src):
         b = k % 4
@@ -176,219 +131,252 @@ def rank_program(g, core, T, topo):
     def picks(out, a, b, win, w0, w1, off, o0, o1):
         return A(sc.activation(out[:, a:b], win[:, w0:w1].indirect(off[:, o0:o1]), Fn.Copy))
 
-    wait("v", "vec", v_blt)
-    v = V(ve.tensor_scalar(T.selo[:, 0:1], T.blt[:, 0:1], 1.0 / 16, float(SEL - 1), Op.mult, Op.min))
-    wait("v", "dtc", cnt["dtc"])
-    lo, hi = slice(0, 64), slice(64, 128)
-    v = V(ve.tensor_copy(T.tcw[hi, t0:t0 + 24], T.tcw[lo, t0:t0 + 24]))
-    v_zz = V(ve.memset(T.zz[:, 12:32], 0.0))
-    wait("v", "vec", v)
-    v = V(ve.tensor_copy(T.tcw[:, SEL:SEL + 16], T.tcw[:, 0:SEL].indirect(T.selo[:, 0:1])))
-    v_wl = V(ve.tensor_copy(T.wl[:], T.tcw[:, t0:t0 + 24]))
-    wait("v", "gpc", p_ef)
-    unit(0, T.ef)
-    wait("v", "vec", v)
-    v = V(ve.tensor_scalar(T.ta[:], T.tcw[:, 0:36], 15, None, Op.bitwise_and))
-    V(ve.tensor_scalar(T.tb[:], T.tcw[:, 0:36], 2047, 4, Op.bitwise_and, Op.logical_shift_right))
-    wait("v", "vec", v)
-    v = V(ve.tensor_scalar(T.tx[:], T.ta[:], 64.0, None, Op.mult))
-    unit(1, T.ef)
-    wait("v", "vec", v)
-    v = V(ve.tensor_tensor(T.ty[:], T.tx[:], T.tb[:], Op.add))
-    unit(2, T.ef)
-    wait("v", "vec", v)
-    wait("v", "act", a_cl)
-    v = V(ve.tensor_tensor(T.tz[:], T.ty[:], T.cl[:], Op.min))
+    def prod(a, b, k, q, s, start, stop, n=HALF):
+        return te.matmul_mx(T["psa" if a else "psb"][:, 512 * b:512 * b + n], T.eq[:, 128 * k:128 * k + 128],
+                            T.es[:, 128 * k:128 * k + 128], T[q][:, a:a + n], T[s][:, a:a + n], start, stop)
 
+    u8, u32 = dt.uint8, dt.uint32
+    one, two = _stages(me)
+    early, late = (0, HALF) if _upper(me) else (HALF, 0)
+    lo, hi = slice(0, 64), slice(64, 128)
+    quads = [slice(32 * k, 32 * k + 32) for k in range(4)]
+    q0, q1 = quads[:2]
+
+    inc("dgr", sy.dma_start(T.grt[:, 0:2 * S], T.gr[:, 0:2 * S]), 16)
+    inc("dgs", sy.dma_start(T.grt[:, 2 * S:4 * S], T.gr[:, 2 * S:4 * S]), 16)
+    for k in range(4):
+        inc("dtc", sc.dma_start(T.tcw[16 * k:16 * k + 16, :], T.tc[:]), 16)
+    for k in range(4):
+        inc("dsn", sy.dma_start(T.snw[16 * k:16 * k + 16, :], T.sn[:]), 16)
+    inc("dwc", sy.dma_start(T.wq[:].bitcast(u8), T.wc[:]), 16)
+    inc("dws", sc.dma_start(T.wqs[:], T.ws[:]), 16)
+
+    v_ef = V(ve.memset(T.ef[:], 0.0))
+    v_en = V(ve.memset(T.en[:], 0.0))
+    iota(T.blk[:, 0:32], [[48, 2], [16, 16]], 0, 3)
+    wait("g", "vec", v_ef)
+    diag = T.ef[:, 3:515:4]
+    p_ef = G(g.affine_select(diag, diag, [[1, 128]], Op.not_equal, 1.0, 0, -1))
+    iota(T.blk[:, 32:64], [[0, 2], [1, 16]], 0)
+    p_blk = iota(T.blk[:, 64:96], [[0, 2], [16, 8], [512, 2]], 0, 4)
+    p_cl = G(g.iota(T.cl[:, 0:3], [[1, 3]], C, 3))
+    p_vals = iota(T.vals[:], [[1, CAP]], -MID, 3)
+
+    V(ve.memset(T.pv[:, ALL:ALL + 16], -3.0))
+    V(ve.memset(T.zz[q0, 12:32], 0.0))
+    after(v_en)
+    V(ve.quantize_mx(T.landq[:, ALL:LAND], T.lands[:, ALL:LAND], T.en[:, 0:512]))
+    wait("v", "gpc", p_ef)
+    for k in range(3):
+        unit(k, T.ef)
+    wait("v", "gpc", p_blk)
+    v_blt = V(ve.transpose(T.blt[:], T.blk[:]))
+    unit(3, T.ef)
+    after(v_blt)
+    V(ve.tensor_scalar(T.selo[:, 0:1], T.blt[:, 0:1], 1.0 / 16, 23.0, Op.mult, Op.min))
+
+    wait("s", "vec", v_en)
+    for i in range(2):
+        a_tab = A(sc.activation(T.tab[:, 512 * i:512 * i + 512], T.en[:, 0:512], Fn.Identity, bias=float(FAR)))
+    wait("s", "vec", v_blt)
+    wait("s", "gpc", p_ef)
+    wait("s", "act", a_tab)
+    a_en = A(sc.activation(T.en[:, 3:515:4], diag, Fn.Copy, scale=-0.125))
+
+    def table_scales(a):
+        wait("s", "dws", cnt["dws"])
+        return picks(T.wsels, a, a + HALF, T.wqs, 0, C, T.wl, a // 16, a // 16 + 12)
+
+    def table_columns(a, scales):
+        wait("v", "dwc", cnt["dwc"])
+        wait("t", "vec", pickc(T.wselq, a, a + HALF, T.wq, 0, C, T.wl, a // 16, a // 16 + 12))
+        wait("t", "act", scales)
+        for b in range(4):
+            prod(a, b, b, "wselq", "wsels", True, False)
+
+    wait("v", "dtc", cnt["dtc"])
+    for half in (lo, hi):
+        v = V(ve.tensor_scalar(T.tu[half, :], T.tcw[lo, :], 2 * C - 1, None, Op.bitwise_and))
     wait("v", "dgr", cnt["dgr"])
-    v_gq = V(ve.quantize_mx(T.gq[:], T.gs[:], T.grt[:]))
+    V(ve.quantize_mx(T.gq[:, 0:S // 2], T.gs[:, 0:S // 2], T.grt[:, 0:2 * S]))
+    wait("v", "dgs", cnt["dgs"])
+    V(ve.quantize_mx(T.gq[:, S // 2:S], T.gs[:, S // 2:S], T.grt[:, 2 * S:4 * S]))
     wait("v", "dsn", cnt["dsn"])
-    V(ve.tensor_copy(T.soff[lo, :], T.snw[lo, :]))
-    v_so = V(ve.tensor_copy(T.soff[hi, :], T.snw[lo, :]))
-    wait("v", "vec", v)
-    v_off = V(ve.tensor_copy(T.off[:], T.tz[:]))
-    wait("v", "vec", v_so)
-    wait("s", "vec", v_so)
+    for half in (lo, hi):
+        v_gq = V(ve.tensor_copy(T.soff[half, :], T.snw[lo, :]))
+    after(v)
+    v = V(ve.tensor_copy(T.mine[:], T.tu[:].indirect(T.selo[:, 0:1])))
+    after(v_gq)
+    wait("s", "vec", v_gq)
     v_p1 = pickc(T.slotq, early, early + HALF, T.gq, 0, S, T.soff, early // 16, early // 16 + 12)
     a_p1 = picks(T.slots, early, early + HALF, T.gs, 0, S, T.soff, early // 16, early // 16 + 12)
-    own, nxt = (0, CAP) if up_ else (CAP, 0)
-    wait("v", "vec", v_off)
-    wait("v", "act", a_vals)
-    v_s1 = V(ve.tensor_copy(T.tab[:].indirect(T.off[:, SEL:SEL + 3]), T.vals[:, own:own + CAP]))
+    after(v)
+    wait("v", "gpc", p_cl)
+    v_wl = V(ve.tensor_scalar(T.wl[:], T.tu[:], float(C - 1), None, Op.min))
+    v = V(ve.tensor_tensor(T.tz[:, 0:3], T.mine[:, 0:3], T.cl[:, 0:3], Op.min))
     v_p2 = pickc(T.slotq, late, late + HALF, T.gq, 0, S, T.soff, late // 16, late // 16 + 12)
-    wait("s", "vec", v_s1)
-    a_pv = A(sc.activation(T.pv[:, z0:z0 + ALL], T.tab[:].indirect(T.off[:, t0:t0 + 24]), Fn.Copy))
     a_p2 = picks(T.slots, late, late + HALF, T.gs, 0, S, T.soff, late // 16, late // 16 + 12)
+    after(v)
+    v = V(ve.tensor_copy(T.off[:, 0:3], T.tz[:, 0:3]))
+    V(ve.tensor_scalar(T.selo[:, 2:3], T.blt[:, 64:65], 1.0 / 16, None, Op.mult))
+    after(v)
+    wait("v", "act", a_en)
+    wait("v", "gpc", p_vals)
+    v_s1 = V(ve.tensor_copy(T.tab[:].indirect(T.off[:, 0:3]), T.vals[:]))
 
     sent = 0
     for stage, vp, ap, cs, ss in ((one, v_p1, a_p1, "arrec", "arres"), (two, v_p2, a_p2, "arrlc", "arrls")):
         for codes in (True, False):
-            eng = _engines(me, stage, T, topo, codes)
             wait("g", "vec" if codes else "act", vp if codes else ap)
-            tr = []
-            for q in stage:
-                rid, pid, _se = topo.addr(T.cores[q])
-                x = CAP * q
-                y = (ZERO if _rising(q) else 0) + CAP * me
-                src, dst = ((T.slotq[:, x:x + CAP].bitcast(u8), T.landq[:, y:y + CAP].bitcast(u8)) if codes
-                            else (T.slots[:, x:x + CAP], T.lands[:, y:y + CAP]))
-                tr.append(RemoteDMATransfer(dst_ids=[DstId(rid=rid, pnc=pid)],
-                                            dma_engine_mask=sum(1 << e for e in eng[q]),
-                                            remote_sem=sem[cs if codes else ss], src=src, dst=dst))
-                sent += len(eng[q])
-            g.remote_dma_fused(tr, local_sem=sem["sent"])
+            sent += _spread(g, core, me, stage, codes, cs if codes else ss, T, topo)
     g.sem_inc(sem["issued"], 1)
-
-    def prod(ps, b, k, q, s, a, start, stop):
-        return te.matmul_mx(T[ps][:, 512 * b:512 * b + HALF], T.eq[:, 128 * k:128 * k + 128],
-                            T.es[:, 128 * k:128 * k + 128], T[q][:, a:a + HALF], T[s][:, a:a + HALF], start, stop)
-
-    parts = (("psa", early), ("psb", late))
-
-    def table_columns(ps, a):
-        wait("v", "dwc", cnt["dwc"])
-        wait("s", "dws", cnt["dws"])
-        wait("t", "vec", pickc(T.wselq, a, a + HALF, T.wq, 0, C, T.wl, a // 16, a // 16 + 12))
-        wait("t", "act", picks(T.wsels, a, a + HALF, T.wqs, 0, C, T.wl, a // 16, a // 16 + 12))
-        for b in range(4):
-            prod(ps, b, b, "wselq", "wsels", a, True, False)
-
-    q0, q1 = slice(0, 32), slice(32, 64)
-    quads = [slice(32 * k, 32 * k + 32) for k in range(4)]
-    unit(3, T.ef)
-    wait("v", "act", a_pv)
-    v = V(ve.transpose(T.pt[:], T.pv[:, z0:z0 + ALL]))
-    v_s2 = V(ve.tensor_copy(T.tab[:].indirect(T.off[:, SEL + 4:SEL + 7]), T.vals[:, nxt:nxt + CAP]))
-    wait("v", "vec", v)
-    v = V(ve.tensor_tensor(T.t1[:], T.pt[:, 0:ALL:32], T.pt[:, 16:ALL:32], Op.add))
-    unit(4, T.en)
-    wait("v", "vec", v)
-    v = V(ve.tensor_tensor(T.t2[lo, :], T.t1[lo, :], T.t1[hi, :], Op.add))
-    wait("v", "vec", v)
-    v = V(ve.tensor_tensor(T.zz[q0, 0:12], T.t2[q0, :], T.t2[q1, :], Op.add))
-    wait("v", "vec", v)
-    for qk in quads[1:]:
-        v = V(ve.tensor_copy(T.zz[qk, 0:12], T.zz[q0, 0:12]))
-    unit(5, T.en)
-    wait("v", "vec", v)
-    v = V(ve.transpose(T.zt[:], T.zz[:]))
-    table_columns(*parts[0])
-    wait("v", "vec", v)
-    wait("v", "act", a_jw)
-    for x, y, n in ((16, 0, 32), (0, 0, 16), (48, 16, 16)):
-        v = V(ve.tensor_tensor(T.dd[:, x:x + n], T.zt[:, y:y + n], T.kk[:, y:y + n], Op.subtract))
-    wait("v", "vec", v)
-    v = V(ve.transpose(T.dr[:], T.dd[:]))
-    v_hy = V(ve.tensor_scalar(T.hy[:], T.dd[:, 16:48], sign / UNIT, 2.0, Op.mult, Op.min))
-    unit(6, T.en)
-    wait("v", "vec", v)
-    wins = ((0, ZERO + HALF) if up_ else (HALF, LAND), (0, LAND))
-    v_pl = []
-    for (ps, a), (w0, w1) in zip(parts, wins):
-        top = w1 - 1 if up_ else ALL - w0
-        for e in range(2):
-            c = 32 * e + a // 32
-            v = V(ve.tensor_scalar(T.pl[:, a // 16 + e:a // 16 + 12:2], T.dr[:, c:c + 6],
-                                   float(MID - sign * shift - w0), float(top), Op.add, Op.min))
-        v_pl.append(v)
-    v_em = unit(7, T.en)
-    table_columns(*parts[1])
+    iota(T.kc[q0, 0:1], [[0, 1]], MID - 6 * FAR, -32)
+    p_pc = iota(T.pc[:], [[HALF, 2], [16, 2]], -MID)
+    p_jw = iota(T.jw[q0, :], [[1, 32]], ALL - MID, 32)
 
     x = CAP * me
     wait("y", "vec", v_p2)
     wait("y", "act", a_p2)
-    inc("down", sy.dma_start(T.landq[:, z0 + x:z0 + x + CAP].bitcast(u8), T.slotq[:, x:x + CAP].bitcast(u8)), 16)
-    inc("down", sy.dma_start(T.lands[:, z0 + x:z0 + x + CAP], T.slots[:, x:x + CAP]), 16)
-    wait("y", "vec", v_s2)
-    for i, qk in enumerate(quads):
-        k = 32 * i + (0 if up_ else 16)
-        inc("dx", sy.dma_start(T.xx[qk, :], T.tab[k:k + 2, 0:C]), 16)
+    inc("down", sy.dma_start(T.landq[:, x:x + CAP].bitcast(u8), T.slotq[:, x:x + CAP].bitcast(u8)), 16)
+    inc("down", sy.dma_start(T.lands[:, x:x + CAP], T.slots[:, x:x + CAP]), 16)
     wait("y", "issued", 1)
-    inc("dfin", sy.dma_start(T.finq[:, old0:old0 + C // 2].bitcast(u8), T.wc[:, 0:2 * C]), 16)
-    wait("y", "vec", v_hy)
+    inc("dfin", sy.dma_start(T.finq[:, ALL:ALL + C // 2].bitcast(u8), T.wc[:, 0:2 * C]), 16)
+
+    def spread(out, src, bias):
+        for x, y, n in ((16, 0, 32), (0, 0, 16), (48, 16, 16)):
+            a = A(sc.activation(out[q0, x:x + n], src[q0, y:y + n], Fn.Identity, bias=bias))
+        wait("s", "act", a)
+        for qk in quads[1:]:
+            a = A(sc.activation(out[qk, :], out[q0, :], Fn.Copy))
+        return a
+
+    wait("s", "vec", v_wl)
+    a_w = table_scales(early)
+    wait("s", "vec", v_s1)
+    a_pv = A(sc.activation(T.pv[:, 0:ALL], T.tab[:, 0:C].indirect(T.wl[:]), Fn.Copy))
+    unit(4, T.en)
+    table_columns(early, a_w)
+    table_columns(late, table_scales(late))
+    wait("v", "act", a_pv)
+    v = V(ve.transpose(T.pt[:], T.pv[:, 0:ALL]))
+    unit(5, T.en)
+    after(v)
+    v = V(ve.tensor_tensor(T.t1[:], T.pt[:, 0:ALL:32], T.pt[:, 16:ALL:32], Op.add))
+    unit(6, T.en)
+    after(v)
+    after(V(ve.tensor_tensor(T.t2[lo, :], T.t1[lo, :], T.t1[hi, :], Op.add)))
+    after(V(ve.tensor_tensor(T.zz[q0, 0:12], T.t2[q0, :], T.t2[q1, :], Op.add)))
+    wait("s", "gpc", p_pc)
+    A(sc.activation(T.pd[:], T.pc[:], Fn.Identity, bias=T.blt[:, 32:33]))
+    wait("s", "vec", V(ve.transpose(T.zt[q0, :], T.zz[q0, :])))
+    a_dd = spread(T.dd, T.zt, T.kc[q0, 0:1])
+    a_hy = A(sc.activation(T.hy[q0, :], T.dd[q0, 16:48], Fn.Sign, bias=float(FAR - MID), scale=-1.0))
+    v_em = unit(7, T.en)
+    after(V(ve.transpose(T.tt[:], T.tab[:, 0:C])))
+    v = V(ve.tensor_tensor(T.x1[:], T.tt[:, 0:C:32], T.tt[:, 16:C:32], Op.min))
+    wait("v", "act", a_dd)
+    w = V(ve.transpose(T.dr[:], T.dd[:]))
+    after(v)
+    after(V(ve.tensor_tensor(T.x2[lo, :], T.x1[lo, :], T.x1[hi, :], Op.min)))
+    for i in (1, 0):
+        for e in range(2):
+            c = 32 * e + 6 * i
+            v_pl = V(ve.tensor_scalar(T.pl[:, 12 * i + e:12 * i + 12:2], T.dr[:, c:c + 6],
+                                      T.pd[:, 2 * i + e:2 * i + e + 1], float(ALL - HALF * i), Op.subtract, Op.min))
+    after(V(ve.tensor_tensor(T.x3[q0, :], T.x2[q0, :], T.x2[q1, :], Op.min)))
+
+    wait("y", "act", a_hy)
     for k in range(4):
-        inc("dup", sy.dma_start(T.pv[32 * k:32 * k + 1, z0:z0 + ALL], T.hy[32 * k:32 * k + 12, :]), 16)
-    inc("dfin", sy.dma_start(T.finq[:, old0 + C // 2:old0 + C].bitcast(u8), T.wc[:, 2 * C:4 * C]), 16)
-    inc("dfin", sy.dma_start(T.fins[:, old0:old0 + C], T.ws[:]), 16)
+        inc("dup", sy.dma_start(T.pv[32 * k:32 * k + 1, 0:ALL], T.hy[0:12, :]), 16)
+    inc("dfin", sy.dma_start(T.finq[:, ALL + C // 2:ALL + C].bitcast(u8), T.wc[:, 2 * C:4 * C]), 16)
+    inc("dfin", sy.dma_start(T.fins[:, ALL:ALL + C], T.ws[:]), 16)
 
-    def arrived(stage, codes):
-        return sum(len(_engines(s, _stages(s)[stage], T, topo, codes)[me])
-                   for s in range(N) if s != me and me in _stages(s)[stage])
+    def landed(qn, stage, codes):
+        n = sum(len(_engines(T.cores[s], _stages(s)[stage], T, topo, codes)[me])
+                for s in range(N) if s != me and me in _stages(s)[stage])
+        wait(qn, (("arres", "arrec"), ("arrls", "arrlc"))[stage][codes], n)
+        if stage:
+            wait(qn, "down", cnt["down"])
 
-    stops = []
-
-    def part(i):
-        (ps, a), (w0, w1) = parts[i], wins[i]
-        cs, ss = ("arrec", "arres") if i == 0 else ("arrlc", "arrls")
-        for qn in "vt":
-            wait(qn, cs, arrived(i, True))
-        for qn in "st":
-            wait(qn, ss, arrived(i, False))
-        if i:
-            for qn in "vst":
-                wait(qn, "down", cnt["down"])
-        wait("v", "vec", v_pl[i])
-        wait("s", "vec", v_pl[i])
-        vp = pickc(T.parq, a, a + HALF, T.landq, w0, w1, T.pl, a // 16, a // 16 + 12)
-        ap = picks(T.pars, a, a + HALF, T.lands, w0, w1, T.pl, a // 16, a // 16 + 12)
-        wait("t", "vec", v_em)
-        if not up_:
-            for b in range(4):
-                prod(ps, b, 4 + b, "landq", "lands", z0 + a, False, False)
-        wait("t", "vec", vp)
-        wait("t", "act", ap)
+    wait("t", "vec", v_em)
+    for stage, a in enumerate((early, late)):
+        landed("t", stage, True)
+        landed("t", stage, False)
         for b in range(4):
-            ins = prod(ps, b, 4 + b, "parq", "pars", a, False, not up_)
-            if up_:
-                ins = prod(ps, b, 4 + b, "landq", "lands", z0 + a, False, True)
-            stops.append(inc("ten", ins))
+            prod(a, b, 4 + b, "landq", "lands", False, False)
 
-    part(0)
-    wait("v", "dx", cnt["dx"])
-    v = V(ve.tensor_tensor(T.xa[lo, :], T.xx[lo, :], T.xx[hi, :], best))
-    wait("v", "vec", v)
-    v = V(ve.tensor_tensor(T.xb[q0, :], T.xa[q0, :], T.xa[q1, :], best))
-    wait("v", "vec", v)
-    v = V(ve.tensor_tensor(T.xc[q0, :], T.xb[q0, :], T.jw[q0, :], best))
-    wait("v", "vec", v)
-    u0, u1 = (nobody, LAND) if up_ else (0, nobody + 16)
-    for k, qk in enumerate(quads):
-        v_up = V(ve.tensor_scalar(T.upg[qk, :], T.xc[q0, 16 * k:16 * k + 16],
-                                  float((ZERO - 1 if up_ else ALL) - MID), float(MID - u0), best, Op.add))
-    part(1)
-    for qk in quads:
-        V(ve.tensor_scalar(T.finl[qk, :], T.xc[q0, :], float(new0 - z0 + MID), None, Op.add))
+    stops = {}
 
-    for i, (ps, a) in enumerate(parts):
-        vl = al = 0
+    def partner_codes(a, n):
+        for stage in range(2):
+            if not a or a == (early, late)[stage]:
+                landed("v", stage, True)
+        after(v_pl)
+        return pickc(T.parq, a, a + n, T.landq, a, LAND, T.pl, a // 16, (a + n) // 16)
+
+    def partner_scales(a, n):
+        for stage in range(2):
+            if not a or a == (early, late)[stage]:
+                landed("s", stage, False)
+        wait("s", "vec", v_pl)
+        return picks(T.pars, a, a + n, T.lands, a, LAND, T.pl, a // 16, (a + n) // 16)
+
+    def partners(a, n, codes, scales):
+        wait("t", "vec", codes)
+        wait("t", "act", scales)
         for b in range(4):
-            out, src = T.h[:, 4 * a + b:4 * (a + HALF):4], T[ps][:, 512 * b:512 * b + HALF]
-            if b % 2:
-                wait("v", "ten", stops[4 * i + b])
-                vl = V(ve.tensor_copy(out, src))
-            else:
-                wait("s", "ten", stops[4 * i + b])
-                al = A(sc.activation(out, src, Fn.Copy))
-        wait("v", "vec", vl)
-        wait("v", "act", al)
-        x = new0 + a
-        v_q = V(ve.quantize_mx(T.finq[:, x:x + HALF], T.fins[:, x:x + HALF], T.h[:, 4 * a:4 * (a + HALF)]))
-        if i == 0:
-            wait("s", "dup", cnt["dup"])
-            wait("s", "vec", v_up)
-            a_up = A(sc.activation(T.upr[:], T.pv[:, u0:u1].indirect(T.upg[:]), Fn.Relu))
-            wait("y", "act", a_up)
-            inc("dout", sy.dma_start(T.up[:], T.upr[0:128:32, :]), 16)
+            stops[a, b] = inc("ten", prod(a, b, 4 + b, "parq", "pars", False, True, n))
 
-    wait("v", "vec", v_q)
-    wait("v", "dfin", cnt["dfin"])
-    wait("s", "vec", v_q)
-    wait("s", "dfin", cnt["dfin"])
-    for j in range(4):
-        vp = pickc(T.outq, 256 * j, 256 * j + 256, T.finq, 0, C + ALL, T.finl, 16 * j, 16 * j + 16)
-        ap = picks(T.outs, 256 * j, 256 * j + 256, T.fins, 0, C + ALL, T.finl, 16 * j, 16 * j + 16)
+    out_of = {"v": 0, "s": 0}
+
+    def leave(a, b, qn):
+        out, src = T.h[:, 4 * a + b:4 * (a + HALF):4], T["psa" if a else "psb"][:, 512 * b:512 * b + HALF]
+        wait(qn, "ten", stops[a, b])
+        out_of[qn] = V(ve.tensor_copy(out, src)) if qn == "v" else A(sc.activation(out, src, Fn.Copy))
+
+    def quantise(a):
+        after(out_of["v"])
+        wait("v", "act", out_of["s"])
+        return V(ve.quantize_mx(T.finq[:, a:a + HALF], T.fins[:, a:a + HALF], T.h[:, 4 * a:4 * (a + HALF)]))
+
+    after(V(ve.transpose(T.xt[q0, :], T.x3[q0, :])))
+    wait("v", "gpc", p_jw)
+    v = V(ve.tensor_tensor(T.xe[q0, :], T.xt[q0, :], T.jw[q0, :], Op.min))
+    n = HALF - CAP
+    partners(HALF, n, partner_codes(HALF, n), partner_scales(HALF, n))
+    partners(0, HALF, partner_codes(0, HALF), partner_scales(0, HALF))
+    wait("s", "vec", v)
+    a_xd = spread(T.xd, T.xe, float(MID))
+    leave(HALF, 0, "v")
+    leave(HALF, 1, "v")
+    wait("v", "act", a_xd)
+    v = V(ve.transpose(T.xr[:], T.xd[:]))
+    leave(HALF, 2, "s")
+    leave(HALF, 3, "s")
+    after(v)
+    v_up = V(ve.tensor_scalar(T.upg[:], T.xr[:].indirect(T.selo[:, 2:3]), float(ALL), None, Op.min))
+    for e in range(2):
+        V(ve.tensor_copy(T.finl[:, e:64:2], T.xr[:, 32 * e:32 * e + 32]))
+    quantise(HALF)
+    for b in range(4):
+        leave(0, b, "sv"[b % 2])
+    v_q = quantise(0)
+    wait("s", "dup", cnt["dup"])
+    wait("s", "vec", v_up)
+    a_up = A(sc.activation(T.upr[:], T.pv[:].indirect(T.upg[:]), Fn.Identity, bias=1.5, scale=0.5))
+    wait("y", "act", a_up)
+    inc("dout", sy.dma_start(T.up[:], T.upr[0:128:32, :]), 16)
+
+    for qn in "vs":
+        wait(qn, "vec", v_q)
+        wait(qn, "dfin", cnt["dfin"])
+    ap = picks(T.outs, 0, C, T.fins, 0, ALL + C, T.finl, 0, C // 16)
+    a = 0
+    for n in PIECES:
+        vp = pickc(T.outq, a, a + n, T.finq, 0, ALL + C, T.finl, a // 16, (a + n) // 16)
         wait("y", "vec", vp)
-        inc("dout", sy.dma_start(T.oc[:, 1024 * j:1024 * j + 1024], T.outq[:, 256 * j:256 * j + 256].bitcast(u8)), 16)
+        inc("dout", sy.dma_start(T.oc[:, 4 * a:4 * (a + n)], T.outq[:, a:a + n].bitcast(u8)), 16)
+        a += n
     wait("s", "act", ap)
     for k in range(4):
         inc("dout", sc.dma_start(T.osc[4 * k:4 * k + 4, :], T.outs[32 * k:32 * k + 4, :]), 16)

@@ -4,10 +4,21 @@ from concourse.mybir import dt, AluOpType as Op, ActivationFunctionType as Fn
 C, S, CAP, N = 1024, 256, 48, 8
 ALL = N * CAP
 HALF = ALL // 2
-LAND = ALL + 128
-MID = LAND // 2
+ZERO = 128
+LAND = ZERO + ALL
 FAR = 1280
-PIECES = (256, 256, 256, 160, 96)
+TURN = 24
+PIECES = (256, 256, 256, 256)
+
+ORDER = {
+    "y": "gr0 gr1 tc1 ws wc own reload up oc ocl osc1",
+    "g": "dx b0 b1 mx cl vals b2 send jw",
+    "v": "ef en diag zq u0 blt u1 selo u2 q0 soff q1 tu p1 tz wl tm off p2 wl2 scat u3 wc1 wc2 tt pt x1 u4 t1 u5 u6 u7 "
+         "x2 blt2 x3 xt gof pl xe pca upd pcb xr ha1 finl ha3 qa hb3 qb last",
+    "s": "sn tc0 pad tab marks m2 en4 s1 s2 ws1 look ws2 rep psa xd2 psb up1 ha0 ha2 hb0 hb1 hb2 up2 lasts osc0",
+    "t": "w1 w2 o1 o2 ma mb",
+}
+SPLIT = False
 
 E4, U8, F32, I32, U16, BF = "float8_e4m3fn_x4", "uint8", "float32", "int32", "uint16", "bfloat16"
 
@@ -20,8 +31,8 @@ SCRATCH = {
     "grt": _sb(4 * S, BF), "gq": _sb(S, E4), "gs": _sb(S, U8),
     "snw": _sb(24, I32), "soff": _sb(24, U16),
     "slotq": _sb(ALL, E4), "slots": _sb(ALL, U8),
-    "landq": _sb(LAND, E4), "lands": _sb(LAND, U8),
-    "ef": _sb(516, BF), "en": _sb(516, BF),
+    "landq": _sb(LAND, E4), "lands": _sb(LAND, U8), "relq": _sb(CAP, E4), "rels": _sb(CAP, U8),
+    "ef": _sb(516, BF), "en": _sb(528, BF), "dx": _sb(128, BF),
     "eq": _sb(1024, E4), "es": _sb(1024, U8),
     "wq": _sb(C, E4), "wqs": _sb(C, U8),
     "finq": _sb(ALL + C, E4), "fins": _sb(ALL + C, U8),
@@ -29,23 +40,27 @@ SCRATCH = {
     "parq": _sb(ALL, E4), "pars": _sb(ALL, U8),
     "h": _sb(4 * ALL, BF),
     "outq": _sb(C, E4), "outs": _sb(C, U8),
-    "tcw": _sb(24, I32), "tu": _sb(24, I32), "mine": _sb(16, I32), "tz": _sb(4, I32), "cl": _sb(4, I32),
-    "off": _sb(4, U16), "wl": _sb(24, U16), "selo": _sb(4, U16),
-    "blk": _sb(96, F32), "blt": _sb(96, F32), "kc": _sb(2, F32), "pc": _sb(4, F32), "pd": _sb(4, F32),
-    "vals": _sb(CAP, BF), "tab": _sb(C + ALL + 16, BF), "pv": _sb(ALL + 16, BF),
-    "pt": _sb(ALL, BF), "t1": _sb(12, F32), "t2": _sb(12, F32), "zz": _sb(32, F32), "zt": _sb(32, F32),
-    "dd": _sb(64, F32), "dr": _sb(64, F32), "pl": _sb(24, U16), "hy": _sb(32, BF),
-    "tt": _sb(C, BF), "x1": _sb(32, F32), "x2": _sb(32, F32), "x3": _sb(32, F32), "xt": _sb(32, F32),
+    "tcw": _sb(24, I32), "tu": _sb(24, I32), "tz": _sb(16, F32), "cl": _sb(16, F32), "tm": _sb(24, F32),
+    "mx": _sb(24, F32), "m1": _sb(24, F32), "m2": _sb(24, F32),
+    "off": _sb(4, U16), "wl": _sb(24, U16), "wl2": _sb(24, U16), "selo": _sb(2, U16), "gof": _sb(4, U16), "rep": _sb(32, F32),
+    "blk": _sb(96, F32), "blt": _sb(96, F32),
+    "vals": _sb(CAP, BF), "marks": _sb(CAP, BF), "tab": _sb(C + 16 + ALL, BF), "pv": _sb(ALL + 32, BF),
+    "pt": _sb(2 * ALL + 32, BF), "pl": _sb(32, U16),
+    "tt": _sb(C, BF), "x1": _sb(96, F32), "x2": _sb(96, F32), "x3": _sb(96, F32), "xt": _sb(64, F32),
     "jw": _sb(32, F32), "xe": _sb(32, F32), "xd": _sb(64, F32), "xr": _sb(64, F32), "finl": _sb(64, U16),
-    "upg": _sb(16, U16), "upr": _sb(256, F32),
+    "upd": _sb(32, F32), "upa": _sb(32, F32), "upb": _sb(32, F32),
     "psa": ("psum", [128, 2048], F32), "psb": ("psum", [128, 2048], F32),
 }
-SEMAPHORES = ["vec", "act", "ten", "gpc", "dsn", "dgr", "dgs", "dtc", "dwc", "dws", "dfin", "down", "dup", "dout",
+SEMAPHORES = ["vec", "act", "ten", "gpc", "dsn", "dgr", "dgs", "dtc", "dwc", "dws", "dfin", "down", "dout",
               "arrec", "arres", "arrlc", "arrls", "sent", "issued"]
 
 
 def _upper(q):
     return q >= N // 2
+
+
+def _base(q):
+    return 0
 
 
 def _stages(s):
@@ -78,7 +93,7 @@ def _spread(g, core, s, stage, codes, name, T, topo):
     eng, tr = _engines(core, stage, T, topo, codes), []
     for q in stage:
         rid, pid, _se = topo.addr(T.cores[q])
-        x, y = CAP * q, CAP * s
+        x, y = CAP * q, _base(q) + CAP * s
         src, dst = ((T.slotq[:, x:x + CAP].bitcast(dt.uint8), T.landq[:, y:y + CAP].bitcast(dt.uint8)) if codes
                     else (T.slots[:, x:x + CAP], T.lands[:, y:y + CAP]))
         tr.append(RemoteDMATransfer(dst_ids=[DstId(rid=rid, pnc=pid)], dma_engine_mask=sum(1 << e for e in eng[q]),
@@ -87,300 +102,293 @@ def _spread(g, core, s, stage, codes, name, T, topo):
     return sum(len(e) for e in eng.values())
 
 
+def _shares(have, keys):
+    size = 1
+    while 2 * size * len(keys) <= len(have):
+        size *= 2
+    spare, out, at = len(have) - size * len(keys), {}, 0
+    for q in keys:
+        n = size
+        if spare >= size:
+            n, spare = 2 * size, spare - size
+        out[q] = have[at:at + n]
+        at += n
+    return out
+
+
+def _helpers(s, T, topo):
+    core = T.cores[s]
+    free = [c for c in topo.cores_of(core) if topo.die(c) != topo.die(core)]
+    out = {}
+    for q in sorted(_stages(s)[1], key=lambda q: sum(topo.may_write(c, T.cores[q]) for c in free)):
+        out[q] = min((c for c in free if c not in out.values() and topo.may_write(c, T.cores[q])),
+                     key=lambda c: sum(topo.may_write(c, d) for d in T.cores))
+    return out
+
+
+def _plan(s, T, topo, codes):
+    core, (one, two), hs = T.cores[s], _stages(s), _helpers(s, T, topo)
+    off = topo.engines(core, T.cores[one[0]])
+    on = [e for e in topo.engines(core, hs[two[0]]) if e not in off]
+    return {**_shares(off, one), **_shares(on, two if codes else two[::-1])}
+
+
+def _write(topo, core, eng, sem, src, dst):
+    rid, pid, _se = topo.addr(core)
+    return RemoteDMATransfer(dst_ids=[DstId(rid=rid, pnc=pid)], dma_engine_mask=sum(1 << e for e in eng),
+                             remote_sem=sem, src=src, dst=dst)
+
+
+def _view(T, name, a, codes):
+    return T[name + "q"][:, a:a + CAP].bitcast(dt.uint8) if codes else T[name + "s"][:, a:a + CAP]
+
+
+def _hand_on(g, core, T, topo):
+    for s in range(N):
+        for q, h in _helpers(s, T, topo).items():
+            if h == core:
+                eng = topo.engines(core, T.cores[q])
+                for codes in (True, False):
+                    g.wait_ge(T.sem["arre" + "sc"[codes]], len(_plan(s, T, topo, codes)[q]))
+                    g.remote_dma_fused([_write(topo, T.cores[q], eng, T.sem["arrl" + "sc"[codes]],
+                                               _view(T, "rel", 0, codes), _view(T, "land", CAP * s, codes))],
+                                       local_sem=T.sem["sent"])
+                g.wait_ge(T.sem["sent"], 2 * len(eng))
+
+
 def rank_program(g, core, T, topo):
     me = T.rank_of(core)
     if me is None:
         return
     sem = T.sem
     ve, sc, te, sy = g.vector, g.scalar, g.tensor, g.sync
-    cnt, seen = {}, {}
-
-    def inc(name, ins, by=1):
-        ins.then_inc(sem[name], by)
-        cnt[name] = cnt.get(name, 0) + by
-        return cnt[name]
-
-    def V(ins):
-        return inc("vec", ins)
-
-    def A(ins):
-        return inc("act", ins)
-
-    def G(ins):
-        return inc("gpc", ins)
-
-    def wait(qn, name, val):
-        if seen.get((qn, name), 0) < val:
-            seen[(qn, name)] = val
-            {"v": ve, "s": sc, "t": te, "y": sy, "g": g}[qn].wait_ge(sem[name], val)
-
-    def after(v):
-        wait("v", "vec", v)
-
-    def iota(out, pattern, base, per=0):
-        return G(g.iota(out, pattern, base, per, allow_small_or_imprecise_dtypes=True))
-
-    def unit(k, src):
-        b = k % 4
-        return V(ve.quantize_mx(T.eq[:, 128 * k:128 * k + 128], T.es[:, 128 * k:128 * k + 128],
-                                src[:, 3 - b:3 - b + 512]))
-
-    def pickc(out, a, b, win, w0, w1, off, o0, o1):
-        return V(ve.tensor_copy(out[:, a:b].bitcast(u32), win[:, w0:w1].bitcast(u32).indirect(off[:, o0:o1])))
-
-    def picks(out, a, b, win, w0, w1, off, o0, o1):
-        return A(sc.activation(out[:, a:b], win[:, w0:w1].indirect(off[:, o0:o1]), Fn.Copy))
-
-    def prod(a, b, k, q, s, start, stop, n=HALF):
-        return te.matmul_mx(T["psa" if a else "psb"][:, 512 * b:512 * b + n], T.eq[:, 128 * k:128 * k + 128],
-                            T.es[:, 128 * k:128 * k + 128], T[q][:, a:a + n], T[s][:, a:a + n], start, stop)
-
+    queue = {"v": ve, "s": sc, "t": te, "y": sy, "g": g}
+    mine = {"v": "vec", "s": "act", "t": "ten", "g": "gpc"}
+    up = False
+    order = ORDER
     u8, u32 = dt.uint8, dt.uint32
-    one, two = _stages(me)
     early, late = (0, HALF) if _upper(me) else (HALF, 0)
+    sign, base = (-1 if up else 1), _base(me)
+    zero = 0 if up else ALL
+    new, old = (C, 0) if up else (0, ALL)
+    window = {HALF: (HALF, LAND), 0: (0, LAND)}
     lo, hi = slice(0, 64), slice(64, 128)
     quads = [slice(32 * k, 32 * k + 32) for k in range(4)]
     q0, q1 = quads[:2]
-
-    inc("dgr", sy.dma_start(T.grt[:, 0:2 * S], T.gr[:, 0:2 * S]), 16)
-    inc("dgs", sy.dma_start(T.grt[:, 2 * S:4 * S], T.gr[:, 2 * S:4 * S]), 16)
-    for k in range(4):
-        inc("dtc", sc.dma_start(T.tcw[16 * k:16 * k + 16, :], T.tc[:]), 16)
-    for k in range(4):
-        inc("dsn", sy.dma_start(T.snw[16 * k:16 * k + 16, :], T.sn[:]), 16)
-    inc("dwc", sy.dma_start(T.wq[:].bitcast(u8), T.wc[:]), 16)
-    inc("dws", sc.dma_start(T.wqs[:], T.ws[:]), 16)
-
-    v_ef = V(ve.memset(T.ef[:], 0.0))
-    v_en = V(ve.memset(T.en[:], 0.0))
-    iota(T.blk[:, 0:32], [[48, 2], [16, 16]], 0, 3)
-    wait("g", "vec", v_ef)
     diag = T.ef[:, 3:515:4]
-    p_ef = G(g.affine_select(diag, diag, [[1, 128]], Op.not_equal, 1.0, 0, -1))
-    iota(T.blk[:, 32:64], [[0, 2], [1, 16]], 0)
-    p_blk = iota(T.blk[:, 64:96], [[0, 2], [16, 8], [512, 2]], 0, 4)
-    p_cl = G(g.iota(T.cl[:, 0:3], [[1, 3]], C, 3))
-    p_vals = iota(T.vals[:], [[1, CAP]], -MID, 3)
 
-    V(ve.memset(T.pv[:, ALL:ALL + 16], -3.0))
-    V(ve.memset(T.zz[q0, 12:32], 0.0))
-    after(v_en)
-    V(ve.quantize_mx(T.landq[:, ALL:LAND], T.lands[:, ALL:LAND], T.en[:, 0:512]))
-    wait("v", "gpc", p_ef)
-    for k in range(3):
-        unit(k, T.ef)
-    wait("v", "gpc", p_blk)
-    v_blt = V(ve.transpose(T.blt[:], T.blk[:]))
-    unit(3, T.ef)
-    after(v_blt)
-    V(ve.tensor_scalar(T.selo[:, 0:1], T.blt[:, 0:1], 1.0 / 16, 23.0, Op.mult, Op.min))
+    steps, done, seen = {}, {}, {}
 
-    wait("s", "vec", v_en)
+    def step(name, needs, *parts, dma=None):
+        steps[name] = (needs.split(), parts, dma)
+
+    def each(f, *args):
+        return lambda: [f(*a) if isinstance(a, tuple) else f(a) for a in args][-1]
+
+    def wait(qn, what):
+        name, val = done[what]
+        if seen.get((qn, name), 0) < val:
+            seen[qn, name] = val
+            queue[qn].wait_ge(sem[name], val)
+
+    def iota(out, pattern, first, per=0):
+        return g.iota(out, pattern, first, per, allow_small_or_imprecise_dtypes=True)
+
+    def pickc(out, a, n, win, off):
+        return ve.tensor_copy(out[:, a:a + n].bitcast(u32), win[:].bitcast(u32).indirect(off[:, a // 16:(a + n) // 16]))
+
+    def picks(out, a, n, win, off):
+        return sc.activation(out[:, a:a + n], win[:].indirect(off[:, a // 16:(a + n) // 16]), Fn.Copy)
+
+    def bank(a, b, n=HALF):
+        return T["psa" if a else "psb"][:, 512 * b:512 * b + n]
+
+    def prod(a, b, k, q, s, start, stop, n=HALF, at=0):
+        return te.matmul_mx(bank(a, b, n), T.eq[:, 128 * k:128 * k + 128], T.es[:, 128 * k:128 * k + 128],
+                            T[q][:, at + a:at + a + n], T[s][:, at + a:at + a + n], start, stop)
+
+    for i, q in enumerate((sc, sy)):
+        step("tc%d" % i, "", *[lambda k=k, q=q: q.dma_start(T.tcw[16 * k:16 * k + 16, :], T.tc[:]) for k in (i, i + 2)],
+             dma="dtc")
+        step("gr%d" % i, "", lambda x=2 * S * i: sy.dma_start(T.grt[:, x:x + 2 * S], T.gr[:, x:x + 2 * S]),
+             dma=("dgr", "dgs")[i])
+    step("sn", "", *[lambda k=k: sc.dma_start(T.snw[16 * k:16 * k + 16, :], T.sn[:]) for k in range(2)], dma="dsn")
+    step("ws", "", lambda: sy.dma_start(T.wqs[:], T.ws[:]), dma="dws")
+    step("wc", "", lambda: sy.dma_start(T.wq[:].bitcast(u8), T.wc[:]), dma="dwc")
+
+    step("ef", "", lambda: ve.memset(T.ef[:], 0.0))
+    step("en", "", lambda: ve.memset(T.en[:], 0.0))
+    step("b0", "", lambda: iota(T.blk[:, 0:32], [[48, 2], [16, 16]], 0, 3))
+    step("b1", "", lambda: iota(T.blk[:, 32:64], [[0, 2], [-2 * sign, 2], [0, 8]], sign))
+    step("b2", "", each(lambda x, s, first: iota(T.blk[:, x:x + 16], [[1, 8], [s, 2]], first), (64, 13, 0), (80, -12, 12)))
+    step("blt", "b0 b1", lambda: ve.transpose(T.blt[:, 0:64], T.blk[:, 0:64]))
+    step("blt2", "b2", lambda: ve.transpose(T.blt[:, 64:96], T.blk[:, 64:96]))
+    step("selo", "blt", lambda: ve.tensor_scalar(T.selo[:, 0:1], T.blt[:, 0:1], 1.0 / 16, 23.0, Op.mult, Op.min))
+    step("gof", "blt2", each(lambda k: ve.tensor_scalar(T.gof[:, 2 * k:2 * k + 1], T.blt[:, 64:65], 6.0 * k, 24.0, Op.add,
+                                                        Op.min), 0, 1))
+    step("dx", "", lambda: iota(T.dx[:], [[1, 128]], 0, -1))
+    step("diag", "ef dx", lambda: ve.tensor_scalar(diag, T.dx[:], 0.0, None, Op.is_equal))
+    step("cl", "", lambda: iota(T.cl[:], [[1, 16]], C + 16, 3))
+    step("vals", "", lambda: iota(T.vals[:], [[1, CAP]], -HALF, 3))
+    step("marks", "vals blt", lambda: sc.activation(T.marks[:], T.vals[:], Fn.Identity, scale=T.blt[:, 32:33]))
+    step("mx", "", lambda: iota(T.mx[:], [[16, N], [0, 3]], 15, -1))
+    step("m2", "mx", lambda: sc.activation(T.m2[:], T.mx[:], Fn.Relu, bias=(64.0 if up else 4.0) * C,
+                                           scale=4.0 * C * sign))
+    step("jw", "", lambda: iota(T.jw[q0, :], [[sign, 32]], sign * (old - new - HALF), 32 * sign))
+    step("tab", "en", each(lambda x, n: sc.activation(T.tab[:, x:x + n], T.en[:, 0:n], Fn.Identity, bias=float(FAR)),
+                           (0, 512), (512, 528)))
+    step("pad", "dx", each(lambda x: sc.activation(T.pv[:, x:x + 16], T.dx[:, 0:16], Fn.Copy), 0, ALL + 16))
+    step("zq", "en", lambda: ve.quantize_mx(T.landq[:, zero:zero + ZERO], T.lands[:, zero:zero + ZERO], T.en[:, 0:512]))
+    step("en4", "zq tab diag", lambda: sc.activation(T.en[:, 3:515:4], diag, Fn.Copy, scale=-0.125))
+    for k in range(8):
+        step("u%d" % k, ("diag", "en4")[k // 4],
+             lambda k=k: ve.quantize_mx(T.eq[:, 128 * k:128 * k + 128], T.es[:, 128 * k:128 * k + 128],
+                                        (T.ef, T.en)[k // 4][:, 3 - k % 4:515 - k % 4]))
+
     for i in range(2):
-        a_tab = A(sc.activation(T.tab[:, 512 * i:512 * i + 512], T.en[:, 0:512], Fn.Identity, bias=float(FAR)))
-    wait("s", "vec", v_blt)
-    wait("s", "gpc", p_ef)
-    wait("s", "act", a_tab)
-    a_en = A(sc.activation(T.en[:, 3:515:4], diag, Fn.Copy, scale=-0.125))
+        step("q%d" % i, "gr%d" % i, lambda x=S // 2 * i: ve.quantize_mx(T.gq[:, x:x + S // 2], T.gs[:, x:x + S // 2],
+                                                                         T.grt[:, 4 * x:4 * x + 2 * S]))
+    step("soff", "sn", each(lambda qk: ve.tensor_copy(T.soff[qk, :], T.snw[q0, :]), *quads))
+    for i, a in ((1, early), (2, late)):
+        step("p%d" % i, "q0 q1 soff", lambda a=a: pickc(T.slotq, a, HALF, T.gq, T.soff))
+        step("s%d" % i, "q0 q1 soff", lambda a=a: picks(T.slots, a, HALF, T.gs, T.soff))
 
-    def table_scales(a):
-        wait("s", "dws", cnt["dws"])
-        return picks(T.wsels, a, a + HALF, T.wqs, 0, C, T.wl, a // 16, a // 16 + 12)
+    def send():
+        sent = 0
+        for stage, owners in enumerate(_stages(me)):
+            for codes in (True, False):
+                wait("g", "sp"[codes] + str(stage + 1))
+                sent += _spread(g, core, me, owners, codes, "arr" + "el"[stage] + "sc"[codes], T, topo)
+        done["sent"] = ("sent", sent)
+        g.sem_inc(sem["issued"], 1)
 
-    def table_columns(a, scales):
-        wait("v", "dwc", cnt["dwc"])
-        wait("t", "vec", pickc(T.wselq, a, a + HALF, T.wq, 0, C, T.wl, a // 16, a // 16 + 12))
-        wait("t", "act", scales)
-        for b in range(4):
-            prod(a, b, b, "wselq", "wsels", True, False)
-
-    wait("v", "dtc", cnt["dtc"])
-    for half in (lo, hi):
-        v = V(ve.tensor_scalar(T.tu[half, :], T.tcw[lo, :], 2 * C - 1, None, Op.bitwise_and))
-    wait("v", "dgr", cnt["dgr"])
-    V(ve.quantize_mx(T.gq[:, 0:S // 2], T.gs[:, 0:S // 2], T.grt[:, 0:2 * S]))
-    wait("v", "dgs", cnt["dgs"])
-    V(ve.quantize_mx(T.gq[:, S // 2:S], T.gs[:, S // 2:S], T.grt[:, 2 * S:4 * S]))
-    wait("v", "dsn", cnt["dsn"])
-    for half in (lo, hi):
-        v_gq = V(ve.tensor_copy(T.soff[half, :], T.snw[lo, :]))
-    after(v)
-    v = V(ve.tensor_copy(T.mine[:], T.tu[:].indirect(T.selo[:, 0:1])))
-    after(v_gq)
-    wait("s", "vec", v_gq)
-    v_p1 = pickc(T.slotq, early, early + HALF, T.gq, 0, S, T.soff, early // 16, early // 16 + 12)
-    a_p1 = picks(T.slots, early, early + HALF, T.gs, 0, S, T.soff, early // 16, early // 16 + 12)
-    after(v)
-    wait("v", "gpc", p_cl)
-    v_wl = V(ve.tensor_scalar(T.wl[:], T.tu[:], float(C - 1), None, Op.min))
-    v = V(ve.tensor_tensor(T.tz[:, 0:3], T.mine[:, 0:3], T.cl[:, 0:3], Op.min))
-    v_p2 = pickc(T.slotq, late, late + HALF, T.gq, 0, S, T.soff, late // 16, late // 16 + 12)
-    a_p2 = picks(T.slots, late, late + HALF, T.gs, 0, S, T.soff, late // 16, late // 16 + 12)
-    after(v)
-    v = V(ve.tensor_copy(T.off[:, 0:3], T.tz[:, 0:3]))
-    V(ve.tensor_scalar(T.selo[:, 2:3], T.blt[:, 64:65], 1.0 / 16, None, Op.mult))
-    after(v)
-    wait("v", "act", a_en)
-    wait("v", "gpc", p_vals)
-    v_s1 = V(ve.tensor_copy(T.tab[:].indirect(T.off[:, 0:3]), T.vals[:]))
-
-    sent = 0
-    for stage, vp, ap, cs, ss in ((one, v_p1, a_p1, "arrec", "arres"), (two, v_p2, a_p2, "arrlc", "arrls")):
+    step("send", "", send)
+    done["issued"] = ("issued", 1)
+    for stage in range(2):
         for codes in (True, False):
-            wait("g", "vec" if codes else "act", vp if codes else ap)
-            sent += _spread(g, core, me, stage, codes, cs if codes else ss, T, topo)
-    g.sem_inc(sem["issued"], 1)
-    iota(T.kc[q0, 0:1], [[0, 1]], MID - 6 * FAR, -32)
-    p_pc = iota(T.pc[:], [[HALF, 2], [16, 2]], -MID)
-    p_jw = iota(T.jw[q0, :], [[1, 32]], ALL - MID, 32)
+            name = "arr" + "el"[stage] + "sc"[codes]
+            done[name] = (name, sum(len(_engines(T.cores[s], _stages(s)[stage], T, topo, codes)[me])
+                                    for s in range(N) if s != me and me in _stages(s)[stage]))
+    src, dst = slice(CAP * me, CAP * me + CAP), slice(base + CAP * me, base + CAP * me + CAP)
+    step("own", "p2 s2 issued", lambda: sy.dma_start(T.landq[:, dst].bitcast(u8), T.slotq[:, src].bitcast(u8)),
+         lambda: sy.dma_start(T.lands[:, dst], T.slots[:, src]), dma="down")
+    step("reload", "issued", lambda: sy.dma_start(T.finq[:, old:old + C].bitcast(u8), T.wc[:]),
+         lambda: sy.dma_start(T.fins[:, old:old + C], T.ws[:]), dma="dfin")
 
-    x = CAP * me
-    wait("y", "vec", v_p2)
-    wait("y", "act", a_p2)
-    inc("down", sy.dma_start(T.landq[:, x:x + CAP].bitcast(u8), T.slotq[:, x:x + CAP].bitcast(u8)), 16)
-    inc("down", sy.dma_start(T.lands[:, x:x + CAP], T.slots[:, x:x + CAP]), 16)
-    wait("y", "issued", 1)
-    inc("dfin", sy.dma_start(T.finq[:, ALL:ALL + C // 2].bitcast(u8), T.wc[:, 0:2 * C]), 16)
+    step("tu", "tc0", each(lambda half: ve.tensor_scalar(T.tu[half, :], T.tcw[lo, :], 2 * C - 1, None,
+                                                         Op.bitwise_and), lo, hi))
+    step("wl", "tu", lambda: ve.tensor_scalar(T.wl[:], T.tu[:], float(C - 1), None, Op.min))
+    step("tz", "tu selo cl", lambda: ve.tensor_tensor(T.tz[:], T.tu[:].indirect(T.selo[:, 0:1]), T.cl[:], Op.min))
+    step("off", "tz", lambda: ve.tensor_copy(T.off[:, 0:3], T.tz[:, 0:3]))
+    step("scat", "off tab marks", lambda: ve.tensor_copy(T.tab[:].indirect(T.off[:, 0:3]), T.marks[:]))
 
-    def spread(out, src, bias):
-        for x, y, n in ((16, 0, 32), (0, 0, 16), (48, 16, 16)):
-            a = A(sc.activation(out[q0, x:x + n], src[q0, y:y + n], Fn.Identity, bias=bias))
-        wait("s", "act", a)
-        for qk in quads[1:]:
-            a = A(sc.activation(out[qk, :], out[q0, :], Fn.Copy))
-        return a
+    step("tm", "tu m2", lambda: ve.tensor_tensor(T.tm[:], T.tu[:], T.m2[:], Op.add))
+    step("wl2", "tm", lambda: ve.tensor_scalar(T.wl2[:], T.tm[:], float(C), None, Op.min))
+    step("look", "scat wl2", lambda: sc.activation(T.pv[:, 16:16 + ALL], T.tab[:, 0:C + 16].indirect(T.wl2[:]), Fn.Copy))
+    step("pt", "look pad", each(lambda x, y, n: ve.transpose(T.pt[:, x:x + n], T.pv[:, y:y + n]),
+                                (0, 16, ALL), (ALL, 0, ALL + 32)))
+    step("tt", "scat", lambda: ve.transpose(T.tt[:], T.tab[:, 0:C]))
+    step("x1", "tt", each(lambda k: ve.tensor_tensor(T.x1[:, 32 * k:32 * k + 32], T.tt[:, 8 * k:C:32],
+                                                     T.tt[:, 8 * k + 16:C:32], Op.min), 0, 1))
+    step("t1", "pt", lambda: ve.tensor_tensor(T.x1[:, 64:89], T.pt[:, 8::32], T.pt[:, 24::32], Op.min))
+    step("x2", "x1 t1", lambda: ve.tensor_tensor(T.x2[lo, 0:89], T.x1[lo, 0:89], T.x1[hi, 0:89], Op.min))
+    step("x3", "x2", lambda: ve.tensor_tensor(T.x3[q0, 0:89], T.x2[q0, 0:89], T.x2[q1, 0:89], Op.min))
+    step("rep", "x3", each(lambda qk: sc.activation(T.rep[qk, 0:25], T.x3[q0, 64:89], Fn.Abs,
+                                                    bias=float(sign * TURN - HALF)), *quads))
 
-    wait("s", "vec", v_wl)
-    a_w = table_scales(early)
-    wait("s", "vec", v_s1)
-    a_pv = A(sc.activation(T.pv[:, 0:ALL], T.tab[:, 0:C].indirect(T.wl[:]), Fn.Copy))
-    unit(4, T.en)
-    table_columns(early, a_w)
-    table_columns(late, table_scales(late))
-    wait("v", "act", a_pv)
-    v = V(ve.transpose(T.pt[:], T.pv[:, 0:ALL]))
-    unit(5, T.en)
-    after(v)
-    v = V(ve.tensor_tensor(T.t1[:], T.pt[:, 0:ALL:32], T.pt[:, 16:ALL:32], Op.add))
-    unit(6, T.en)
-    after(v)
-    after(V(ve.tensor_tensor(T.t2[lo, :], T.t1[lo, :], T.t1[hi, :], Op.add)))
-    after(V(ve.tensor_tensor(T.zz[q0, 0:12], T.t2[q0, :], T.t2[q1, :], Op.add)))
-    wait("s", "gpc", p_pc)
-    A(sc.activation(T.pd[:], T.pc[:], Fn.Identity, bias=T.blt[:, 32:33]))
-    wait("s", "vec", V(ve.transpose(T.zt[q0, :], T.zz[q0, :])))
-    a_dd = spread(T.dd, T.zt, T.kc[q0, 0:1])
-    a_hy = A(sc.activation(T.hy[q0, :], T.dd[q0, 16:48], Fn.Sign, bias=float(FAR - MID), scale=-1.0))
-    v_em = unit(7, T.en)
-    after(V(ve.transpose(T.tt[:], T.tab[:, 0:C])))
-    v = V(ve.tensor_tensor(T.x1[:], T.tt[:, 0:C:32], T.tt[:, 16:C:32], Op.min))
-    wait("v", "act", a_dd)
-    w = V(ve.transpose(T.dr[:], T.dd[:]))
-    after(v)
-    after(V(ve.tensor_tensor(T.x2[lo, :], T.x1[lo, :], T.x1[hi, :], Op.min)))
-    for i in (1, 0):
-        for e in range(2):
-            c = 32 * e + 6 * i
-            v_pl = V(ve.tensor_scalar(T.pl[:, 12 * i + e:12 * i + 12:2], T.dr[:, c:c + 6],
-                                      T.pd[:, 2 * i + e:2 * i + e + 1], float(ALL - HALF * i), Op.subtract, Op.min))
-    after(V(ve.tensor_tensor(T.x3[q0, :], T.x2[q0, :], T.x2[q1, :], Op.min)))
+    def partners(k):
+        w0 = window[HALF * k][0]
+        ops = (-1.0, float(LAND), Op.mult, Op.add) if up else (float(w0), float(ALL - w0), Op.subtract, Op.min)
+        return ve.tensor_scalar(T.pl[:, 16 * k:16 * k + 16], T.rep[:, 0:25].indirect(T.gof[:, 2 * k:2 * k + 1]), *ops)
 
-    wait("y", "act", a_hy)
-    for k in range(4):
-        inc("dup", sy.dma_start(T.pv[32 * k:32 * k + 1, 0:ALL], T.hy[0:12, :]), 16)
-    inc("dfin", sy.dma_start(T.finq[:, ALL + C // 2:ALL + C].bitcast(u8), T.wc[:, 2 * C:4 * C]), 16)
-    inc("dfin", sy.dma_start(T.fins[:, ALL:ALL + C], T.ws[:]), 16)
+    step("pl", "rep gof", each(partners, 0, 1))
 
-    def landed(qn, stage, codes):
-        n = sum(len(_engines(T.cores[s], _stages(s)[stage], T, topo, codes)[me])
-                for s in range(N) if s != me and me in _stages(s)[stage])
-        wait(qn, (("arres", "arrec"), ("arrls", "arrlc"))[stage][codes], n)
-        if stage:
-            wait(qn, "down", cnt["down"])
+    step("xt", "x3", lambda: ve.transpose(T.xt[q0, :], T.x3[q0, 0:64]))
+    step("xe", "xt jw", each(lambda x, y, n: ve.tensor_tensor(T.xd[q0, x:x + n], T.xt[q0, y:y + n], T.jw[q0, y:y + n],
+                                                              Op.min), (16, 0, 32), (0, 0, 16), (48, 16, 16)))
+    step("xd2", "xe", each(lambda qk: sc.activation(T.xd[qk, :], T.xd[q0, :], Fn.Copy), *quads[1:]))
+    step("xr", "xd2", lambda: ve.transpose(T.xr[:], T.xd[:]))
+    step("finl", "xr", each(lambda e: ve.tensor_scalar(T.finl[:, e:64:2], T.xr[:, 32 * e:32 * e + 32], float(HALF), None,
+                                                       Op.add), 0, 1))
+    step("upd", "xt", lambda: ve.tensor_tensor(T.upd[q0, :], T.xt[q0, 0:32], T.xt[q0, 32:64], Op.add))
+    step("up1", "upd", lambda: sc.activation(T.upa[q0, :], T.upd[q0, :], Fn.Relu, bias=sign * TURN + 1.0))
+    step("up2", "up1", lambda: sc.activation(T.upb[q0, :], T.upa[q0, :], Fn.Relu, bias=2.0, scale=-1.0))
+    step("up", "up2", lambda: sy.dma_start(T.up[:], T.upb[q0, :]), dma="dout")
 
-    wait("t", "vec", v_em)
-    for stage, a in enumerate((early, late)):
-        landed("t", stage, True)
-        landed("t", stage, False)
+    def partner(qn, out, win, a, x, n, cast=lambda v: v):
+        (w0, w1), o = window[a], a // 12 + x // 16
+        src = cast(win[:, w0:w1]).indirect(T.pl[:, o:o + n // 16])
+        dst = cast(out[:, a + x:a + x + n])
+        return ve.tensor_copy(dst, src) if qn == "v" else sc.activation(dst, src, Fn.Copy)
+
+    for h, a in (("a", HALF), ("b", 0)):
+        k = "1" if a == early else "2"
+        n = HALF - CAP if a else HALF
+        here = "arrec arres" if a == early else "arrlc arrls own"
+        codes, scales = ("arrec", "arres") if a == early == HALF else ("arrec arrlc own", "arres arrls own")
+        cut = ((0, n),)
+        step("wc" + k, "wc wl", lambda a=a: pickc(T.wselq, a, HALF, T.wq, T.wl))
+        step("ws" + k, "ws wl", lambda a=a: picks(T.wsels, a, HALF, T.wqs, T.wl))
+        step("w" + k, "wc%s ws%s u0 u1 u2 u3" % (k, k),
+             each(lambda b, a=a: prod(a, b, b, "wselq", "wsels", True, False), 0, 1, 2, 3))
+        step("o" + k, "u4 u5 u6 u7 " + here,
+             each(lambda b, a=a: prod(a, b, 4 + b, "landq", "lands", False, False), 0, 1, 2, 3))
+        step("pc" + h, "pl zq " + codes,
+             each(lambda x, n, a=a: partner("v", T.parq, T.landq, a, x, n, lambda v: v.bitcast(u32)), *cut))
+        step("ps" + h, "pl zq " + scales, lambda a=a, c=cut[0]: partner("s", T.pars, T.lands, a, *c))
+        step("pv" + h, "pl zq " + scales, lambda a=a, c=cut[-1]: partner("v", T.pars, T.lands, a, *c))
+
+        def rest(b, a=a, n=n):
+            ins = prod(a, b, 4 + b, "parq", "pars", False, not up, n)
+            return prod(a, b, 4 + b, "landq", "lands", False, True, at=base) if up else ins
+
+        step("m" + h, "u4 u5 u6 u7 pc%s ps%s" % (h, h) + (" pv" + h) * (len(cut) - 1),
+             *[lambda b=b, f=rest: f(b) for b in range(4)])
         for b in range(4):
-            prod(a, b, 4 + b, "landq", "lands", False, False)
+            out, on = T.h[:, 4 * a + b:4 * (a + HALF):4], "h%s%d" % (h, b)
+            step(on, "m%s.%d" % (h, b), (lambda o=out, i=bank(a, b): ve.tensor_copy(o, i)) if on in order["v"].split()
+                 else (lambda o=out, i=bank(a, b): sc.activation(o, i, Fn.Copy)))
+        step("q" + h, " ".join("h%s%d" % (h, b) for b in range(4)),
+             lambda a=a: ve.quantize_mx(T.finq[:, new + a:new + a + HALF], T.fins[:, new + a:new + a + HALF],
+                                        T.h[:, 4 * a:4 * (a + HALF)]))
 
-    stops = {}
+    runs = [(sum(PIECES[:i]), n) for i, n in enumerate(PIECES)]
+    step("last", "qa qb finl reload", *[lambda a=a, n=n: pickc(T.outq, a, n, T.finq, T.finl) for a, n in runs])
+    step("lasts", "qa qb finl reload", lambda: picks(T.outs, 0, C, T.fins, T.finl))
 
-    def partner_codes(a, n):
-        for stage in range(2):
-            if not a or a == (early, late)[stage]:
-                landed("v", stage, True)
-        after(v_pl)
-        return pickc(T.parq, a, a + n, T.landq, a, LAND, T.pl, a // 16, (a + n) // 16)
+    def store(i):
+        a, n = runs[i]
+        wait("y", "last.%d" % i)
+        return sy.dma_start(T.oc[:, 4 * a:4 * (a + n)], T.outq[:, a:a + n].bitcast(u8))
 
-    def partner_scales(a, n):
-        for stage in range(2):
-            if not a or a == (early, late)[stage]:
-                landed("s", stage, False)
-        wait("s", "vec", v_pl)
-        return picks(T.pars, a, a + n, T.lands, a, LAND, T.pl, a // 16, (a + n) // 16)
+    step("oc", "", *[lambda i=i: store(i) for i in range(len(runs) - 1)], dma="dout")
+    step("ocl", "", lambda: store(len(runs) - 1), dma="dout")
+    for i, q in enumerate((sc, sy)):
+        step("osc%d" % i, "lasts", *[lambda k=k, q=q: q.dma_start(T.osc[4 * k:4 * k + 4, :], T.outs[32 * k:32 * k + 4, :])
+                                     for k in (i, i + 2)], dma="dout")
 
-    def partners(a, n, codes, scales):
-        wait("t", "vec", codes)
-        wait("t", "act", scales)
-        for b in range(4):
-            stops[a, b] = inc("ten", prod(a, b, 4 + b, "parq", "pars", False, True, n))
+    cnt = {}
+    for qn, names in order.items():
+        for name in names.split():
+            _needs, parts, dma = steps[name]
+            if name != "send":
+                for i in range(len(parts)):
+                    s = dma or mine[qn]
+                    cnt[s] = cnt.get(s, 0) + (16 if dma else 1)
+                    done[name] = done["%s.%d" % (name, i)] = (s, cnt[s])
+    for name, (_needs, _parts, dma) in steps.items():
+        if dma:
+            done[name] = (dma, cnt[dma])
+    for qn, names in order.items():
+        for name in names.split():
+            needs, parts, dma = steps[name]
+            for what in needs:
+                wait(qn, what)
+            for part in parts:
+                ins = part()
+                if name != "send":
+                    ins.then_inc(sem[dma or mine[qn]], 16 if dma else 1)
 
-    out_of = {"v": 0, "s": 0}
-
-    def leave(a, b, qn):
-        out, src = T.h[:, 4 * a + b:4 * (a + HALF):4], T["psa" if a else "psb"][:, 512 * b:512 * b + HALF]
-        wait(qn, "ten", stops[a, b])
-        out_of[qn] = V(ve.tensor_copy(out, src)) if qn == "v" else A(sc.activation(out, src, Fn.Copy))
-
-    def quantise(a):
-        after(out_of["v"])
-        wait("v", "act", out_of["s"])
-        return V(ve.quantize_mx(T.finq[:, a:a + HALF], T.fins[:, a:a + HALF], T.h[:, 4 * a:4 * (a + HALF)]))
-
-    after(V(ve.transpose(T.xt[q0, :], T.x3[q0, :])))
-    wait("v", "gpc", p_jw)
-    v = V(ve.tensor_tensor(T.xe[q0, :], T.xt[q0, :], T.jw[q0, :], Op.min))
-    n = HALF - CAP
-    partners(HALF, n, partner_codes(HALF, n), partner_scales(HALF, n))
-    partners(0, HALF, partner_codes(0, HALF), partner_scales(0, HALF))
-    wait("s", "vec", v)
-    a_xd = spread(T.xd, T.xe, float(MID))
-    leave(HALF, 0, "v")
-    leave(HALF, 1, "v")
-    wait("v", "act", a_xd)
-    v = V(ve.transpose(T.xr[:], T.xd[:]))
-    leave(HALF, 2, "s")
-    leave(HALF, 3, "s")
-    after(v)
-    v_up = V(ve.tensor_scalar(T.upg[:], T.xr[:].indirect(T.selo[:, 2:3]), float(ALL), None, Op.min))
-    for e in range(2):
-        V(ve.tensor_copy(T.finl[:, e:64:2], T.xr[:, 32 * e:32 * e + 32]))
-    quantise(HALF)
-    for b in range(4):
-        leave(0, b, "sv"[b % 2])
-    v_q = quantise(0)
-    wait("s", "dup", cnt["dup"])
-    wait("s", "vec", v_up)
-    a_up = A(sc.activation(T.upr[:], T.pv[:].indirect(T.upg[:]), Fn.Identity, bias=1.5, scale=0.5))
-    wait("y", "act", a_up)
-    inc("dout", sy.dma_start(T.up[:], T.upr[0:128:32, :]), 16)
-
-    for qn in "vs":
-        wait(qn, "vec", v_q)
-        wait(qn, "dfin", cnt["dfin"])
-    ap = picks(T.outs, 0, C, T.fins, 0, ALL + C, T.finl, 0, C // 16)
-    a = 0
-    for n in PIECES:
-        vp = pickc(T.outq, a, a + n, T.finq, 0, ALL + C, T.finl, a // 16, (a + n) // 16)
-        wait("y", "vec", vp)
-        inc("dout", sy.dma_start(T.oc[:, 4 * a:4 * (a + n)], T.outq[:, a:a + n].bitcast(u8)), 16)
-        a += n
-    wait("s", "act", ap)
-    for k in range(4):
-        inc("dout", sc.dma_start(T.osc[4 * k:4 * k + 4, :], T.outs[32 * k:32 * k + 4, :]), 16)
-
-    wait("g", "sent", sent)
+    wait("g", "sent")
     for name in ("vec", "act", "ten", "gpc", "dout"):
-        wait("g", name, cnt[name])
+        g.wait_ge(sem[name], cnt[name])

from concourse.bass import DstId, RemoteDMATransfer
from concourse.mybir import dt, AluOpType as Op, ActivationFunctionType as Fn

C, S, CAP, N = 1024, 256, 48, 8
ALL = N * CAP
HALF = ALL // 2
ZERO = 128
LAND = ZERO + ALL
FAR = 1280
TURN = 24
PIECES = (256, 256, 256, 256)

ORDER = {
    "y": "gr0 gr1 tc1 ws wc own reload up oc ocl osc1",
    "g": "dx b0 b1 mx cl vals b2 send jw",
    "v": "ef en diag zq u0 blt u1 selo u2 q0 soff q1 tu p1 tz wl tm off p2 wl2 scat u3 wc1 wc2 tt pt x1 u4 t1 u5 u6 u7 "
         "x2 blt2 x3 xt gof pl xe pca upd pcb xr ha1 finl ha3 qa hb3 qb last",
    "s": "sn tc0 pad tab marks m2 en4 s1 s2 ws1 look ws2 rep psa xd2 psb up1 ha0 ha2 hb0 hb1 hb2 up2 lasts osc0",
    "t": "w1 w2 o1 o2 ma mb",
}
SPLIT = False

E4, U8, F32, I32, U16, BF = "float8_e4m3fn_x4", "uint8", "float32", "int32", "uint16", "bfloat16"


def _sb(n, d):
    return ("sbuf", [128, n], d)


SCRATCH = {
    "grt": _sb(4 * S, BF), "gq": _sb(S, E4), "gs": _sb(S, U8),
    "snw": _sb(24, I32), "soff": _sb(24, U16),
    "slotq": _sb(ALL, E4), "slots": _sb(ALL, U8),
    "landq": _sb(LAND, E4), "lands": _sb(LAND, U8), "relq": _sb(CAP, E4), "rels": _sb(CAP, U8),
    "ef": _sb(516, BF), "en": _sb(528, BF), "dx": _sb(128, BF),
    "eq": _sb(1024, E4), "es": _sb(1024, U8),
    "wq": _sb(C, E4), "wqs": _sb(C, U8),
    "finq": _sb(ALL + C, E4), "fins": _sb(ALL + C, U8),
    "wselq": _sb(ALL, E4), "wsels": _sb(ALL, U8),
    "parq": _sb(ALL, E4), "pars": _sb(ALL, U8),
    "h": _sb(4 * ALL, BF),
    "outq": _sb(C, E4), "outs": _sb(C, U8),
    "tcw": _sb(24, I32), "tu": _sb(24, I32), "tz": _sb(16, F32), "cl": _sb(16, F32), "tm": _sb(24, F32),
    "mx": _sb(24, F32), "m1": _sb(24, F32), "m2": _sb(24, F32),
    "off": _sb(4, U16), "wl": _sb(24, U16), "wl2": _sb(24, U16), "selo": _sb(2, U16), "gof": _sb(4, U16), "rep": _sb(32, F32),
    "blk": _sb(96, F32), "blt": _sb(96, F32),
    "vals": _sb(CAP, BF), "marks": _sb(CAP, BF), "tab": _sb(C + 16 + ALL, BF), "pv": _sb(ALL + 32, BF),
    "pt": _sb(2 * ALL + 32, BF), "pl": _sb(32, U16),
    "tt": _sb(C, BF), "x1": _sb(96, F32), "x2": _sb(96, F32), "x3": _sb(96, F32), "xt": _sb(64, F32),
    "jw": _sb(32, F32), "xe": _sb(32, F32), "xd": _sb(64, F32), "xr": _sb(64, F32), "finl": _sb(64, U16),
    "upd": _sb(32, F32), "upa": _sb(32, F32), "upb": _sb(32, F32),
    "psa": ("psum", [128, 2048], F32), "psb": ("psum", [128, 2048], F32),
}
SEMAPHORES = ["vec", "act", "ten", "gpc", "dsn", "dgr", "dgs", "dtc", "dwc", "dws", "dfin", "down", "dout",
              "arrec", "arres", "arrlc", "arrls", "sent", "issued"]


def _upper(q):
    return q >= N // 2


def _base(q):
    return 0


def _stages(s):
    return ([q for q in range(N) if _upper(q) != _upper(s)],
            [q for q in range(N) if _upper(q) == _upper(s) and q != s])


def _engines(src, stage, T, topo, codes):
    have = topo.engines(src, T.cores[stage[0]])
    size = 1
    while 2 * size * len(stage) <= len(have):
        size *= 2
    spare = len(have) - size * len(stage)

    def far(q):
        a, b = topo.chip(src), topo.chip(T.cores[q])
        return not topo.mates(a, b) and not topo.same_plane(a, b)

    out, at = {}, 0
    for q in sorted(stage, key=far, reverse=not codes):
        n = size
        if spare >= size and far(q):
            n, spare = 2 * size, spare - size
        out[q] = have[at:at + n]
        at += n
    return out


def _spread(g, core, s, stage, codes, name, T, topo):
    eng, tr = _engines(core, stage, T, topo, codes), []
    for q in stage:
        rid, pid, _se = topo.addr(T.cores[q])
        x, y = CAP * q, _base(q) + CAP * s
        src, dst = ((T.slotq[:, x:x + CAP].bitcast(dt.uint8), T.landq[:, y:y + CAP].bitcast(dt.uint8)) if codes
                    else (T.slots[:, x:x + CAP], T.lands[:, y:y + CAP]))
        tr.append(RemoteDMATransfer(dst_ids=[DstId(rid=rid, pnc=pid)], dma_engine_mask=sum(1 << e for e in eng[q]),
                                    remote_sem=T.sem[name], src=src, dst=dst))
    g.remote_dma_fused(tr, local_sem=T.sem["sent"])
    return sum(len(e) for e in eng.values())


def _shares(have, keys):
    size = 1
    while 2 * size * len(keys) <= len(have):
        size *= 2
    spare, out, at = len(have) - size * len(keys), {}, 0
    for q in keys:
        n = size
        if spare >= size:
            n, spare = 2 * size, spare - size
        out[q] = have[at:at + n]
        at += n
    return out


def _helpers(s, T, topo):
    core = T.cores[s]
    free = [c for c in topo.cores_of(core) if topo.die(c) != topo.die(core)]
    out = {}
    for q in sorted(_stages(s)[1], key=lambda q: sum(topo.may_write(c, T.cores[q]) for c in free)):
        out[q] = min((c for c in free if c not in out.values() and topo.may_write(c, T.cores[q])),
                     key=lambda c: sum(topo.may_write(c, d) for d in T.cores))
    return out


def _plan(s, T, topo, codes):
    core, (one, two), hs = T.cores[s], _stages(s), _helpers(s, T, topo)
    off = topo.engines(core, T.cores[one[0]])
    on = [e for e in topo.engines(core, hs[two[0]]) if e not in off]
    return {**_shares(off, one), **_shares(on, two if codes else two[::-1])}


def _write(topo, core, eng, sem, src, dst):
    rid, pid, _se = topo.addr(core)
    return RemoteDMATransfer(dst_ids=[DstId(rid=rid, pnc=pid)], dma_engine_mask=sum(1 << e for e in eng),
                             remote_sem=sem, src=src, dst=dst)


def _view(T, name, a, codes):
    return T[name + "q"][:, a:a + CAP].bitcast(dt.uint8) if codes else T[name + "s"][:, a:a + CAP]


def _hand_on(g, core, T, topo):
    for s in range(N):
        for q, h in _helpers(s, T, topo).items():
            if h == core:
                eng = topo.engines(core, T.cores[q])
                for codes in (True, False):
                    g.wait_ge(T.sem["arre" + "sc"[codes]], len(_plan(s, T, topo, codes)[q]))
                    g.remote_dma_fused([_write(topo, T.cores[q], eng, T.sem["arrl" + "sc"[codes]],
                                               _view(T, "rel", 0, codes), _view(T, "land", CAP * s, codes))],
                                       local_sem=T.sem["sent"])
                g.wait_ge(T.sem["sent"], 2 * len(eng))


def rank_program(g, core, T, topo):
    me = T.rank_of(core)
    if me is None:
        return
    sem = T.sem
    ve, sc, te, sy = g.vector, g.scalar, g.tensor, g.sync
    queue = {"v": ve, "s": sc, "t": te, "y": sy, "g": g}
    mine = {"v": "vec", "s": "act", "t": "ten", "g": "gpc"}
    up = False
    order = ORDER
    u8, u32 = dt.uint8, dt.uint32
    early, late = (0, HALF) if _upper(me) else (HALF, 0)
    sign, base = (-1 if up else 1), _base(me)
    zero = 0 if up else ALL
    new, old = (C, 0) if up else (0, ALL)
    window = {HALF: (HALF, LAND), 0: (0, LAND)}
    lo, hi = slice(0, 64), slice(64, 128)
    quads = [slice(32 * k, 32 * k + 32) for k in range(4)]
    q0, q1 = quads[:2]
    diag = T.ef[:, 3:515:4]

    steps, done, seen = {}, {}, {}

    def step(name, needs, *parts, dma=None):
        steps[name] = (needs.split(), parts, dma)

    def each(f, *args):
        return lambda: [f(*a) if isinstance(a, tuple) else f(a) for a in args][-1]

    def wait(qn, what):
        name, val = done[what]
        if seen.get((qn, name), 0) < val:
            seen[qn, name] = val
            queue[qn].wait_ge(sem[name], val)

    def iota(out, pattern, first, per=0):
        return g.iota(out, pattern, first, per, allow_small_or_imprecise_dtypes=True)

    def pickc(out, a, n, win, off):
        return ve.tensor_copy(out[:, a:a + n].bitcast(u32), win[:].bitcast(u32).indirect(off[:, a // 16:(a + n) // 16]))

    def picks(out, a, n, win, off):
        return sc.activation(out[:, a:a + n], win[:].indirect(off[:, a // 16:(a + n) // 16]), Fn.Copy)

    def bank(a, b, n=HALF):
        return T["psa" if a else "psb"][:, 512 * b:512 * b + n]

    def prod(a, b, k, q, s, start, stop, n=HALF, at=0):
        return te.matmul_mx(bank(a, b, n), T.eq[:, 128 * k:128 * k + 128], T.es[:, 128 * k:128 * k + 128],
                            T[q][:, at + a:at + a + n], T[s][:, at + a:at + a + n], start, stop)

    for i, q in enumerate((sc, sy)):
        step("tc%d" % i, "", *[lambda k=k, q=q: q.dma_start(T.tcw[16 * k:16 * k + 16, :], T.tc[:]) for k in (i, i + 2)],
             dma="dtc")
        step("gr%d" % i, "", lambda x=2 * S * i: sy.dma_start(T.grt[:, x:x + 2 * S], T.gr[:, x:x + 2 * S]),
             dma=("dgr", "dgs")[i])
    step("sn", "", *[lambda k=k: sc.dma_start(T.snw[16 * k:16 * k + 16, :], T.sn[:]) for k in range(2)], dma="dsn")
    step("ws", "", lambda: sy.dma_start(T.wqs[:], T.ws[:]), dma="dws")
    step("wc", "", lambda: sy.dma_start(T.wq[:].bitcast(u8), T.wc[:]), dma="dwc")

    step("ef", "", lambda: ve.memset(T.ef[:], 0.0))
    step("en", "", lambda: ve.memset(T.en[:], 0.0))
    step("b0", "", lambda: iota(T.blk[:, 0:32], [[48, 2], [16, 16]], 0, 3))
    step("b1", "", lambda: iota(T.blk[:, 32:64], [[0, 2], [-2 * sign, 2], [0, 8]], sign))
    step("b2", "", each(lambda x, s, first: iota(T.blk[:, x:x + 16], [[1, 8], [s, 2]], first), (64, 13, 0), (80, -12, 12)))
    step("blt", "b0 b1", lambda: ve.transpose(T.blt[:, 0:64], T.blk[:, 0:64]))
    step("blt2", "b2", lambda: ve.transpose(T.blt[:, 64:96], T.blk[:, 64:96]))
    step("selo", "blt", lambda: ve.tensor_scalar(T.selo[:, 0:1], T.blt[:, 0:1], 1.0 / 16, 23.0, Op.mult, Op.min))
    step("gof", "blt2", each(lambda k: ve.tensor_scalar(T.gof[:, 2 * k:2 * k + 1], T.blt[:, 64:65], 6.0 * k, 24.0, Op.add,
                                                        Op.min), 0, 1))
    step("dx", "", lambda: iota(T.dx[:], [[1, 128]], 0, -1))
    step("diag", "ef dx", lambda: ve.tensor_scalar(diag, T.dx[:], 0.0, None, Op.is_equal))
    step("cl", "", lambda: iota(T.cl[:], [[1, 16]], C + 16, 3))
    step("vals", "", lambda: iota(T.vals[:], [[1, CAP]], -HALF, 3))
    step("marks", "vals blt", lambda: sc.activation(T.marks[:], T.vals[:], Fn.Identity, scale=T.blt[:, 32:33]))
    step("mx", "", lambda: iota(T.mx[:], [[16, N], [0, 3]], 15, -1))
    step("m2", "mx", lambda: sc.activation(T.m2[:], T.mx[:], Fn.Relu, bias=(64.0 if up else 4.0) * C,
                                           scale=4.0 * C * sign))
    step("jw", "", lambda: iota(T.jw[q0, :], [[sign, 32]], sign * (old - new - HALF), 32 * sign))
    step("tab", "en", each(lambda x, n: sc.activation(T.tab[:, x:x + n], T.en[:, 0:n], Fn.Identity, bias=float(FAR)),
                           (0, 512), (512, 528)))
    step("pad", "dx", each(lambda x: sc.activation(T.pv[:, x:x + 16], T.dx[:, 0:16], Fn.Copy), 0, ALL + 16))
    step("zq", "en", lambda: ve.quantize_mx(T.landq[:, zero:zero + ZERO], T.lands[:, zero:zero + ZERO], T.en[:, 0:512]))
    step("en4", "zq tab diag", lambda: sc.activation(T.en[:, 3:515:4], diag, Fn.Copy, scale=-0.125))
    for k in range(8):
        step("u%d" % k, ("diag", "en4")[k // 4],
             lambda k=k: ve.quantize_mx(T.eq[:, 128 * k:128 * k + 128], T.es[:, 128 * k:128 * k + 128],
                                        (T.ef, T.en)[k // 4][:, 3 - k % 4:515 - k % 4]))

    for i in range(2):
        step("q%d" % i, "gr%d" % i, lambda x=S // 2 * i: ve.quantize_mx(T.gq[:, x:x + S // 2], T.gs[:, x:x + S // 2],
                                                                         T.grt[:, 4 * x:4 * x + 2 * S]))
    step("soff", "sn", each(lambda qk: ve.tensor_copy(T.soff[qk, :], T.snw[q0, :]), *quads))
    for i, a in ((1, early), (2, late)):
        step("p%d" % i, "q0 q1 soff", lambda a=a: pickc(T.slotq, a, HALF, T.gq, T.soff))
        step("s%d" % i, "q0 q1 soff", lambda a=a: picks(T.slots, a, HALF, T.gs, T.soff))

    def send():
        sent = 0
        for stage, owners in enumerate(_stages(me)):
            for codes in (True, False):
                wait("g", "sp"[codes] + str(stage + 1))
                sent += _spread(g, core, me, owners, codes, "arr" + "el"[stage] + "sc"[codes], T, topo)
        done["sent"] = ("sent", sent)
        g.sem_inc(sem["issued"], 1)

    step("send", "", send)
    done["issued"] = ("issued", 1)
    for stage in range(2):
        for codes in (True, False):
            name = "arr" + "el"[stage] + "sc"[codes]
            done[name] = (name, sum(len(_engines(T.cores[s], _stages(s)[stage], T, topo, codes)[me])
                                    for s in range(N) if s != me and me in _stages(s)[stage]))
    src, dst = slice(CAP * me, CAP * me + CAP), slice(base + CAP * me, base + CAP * me + CAP)
    step("own", "p2 s2 issued", lambda: sy.dma_start(T.landq[:, dst].bitcast(u8), T.slotq[:, src].bitcast(u8)),
         lambda: sy.dma_start(T.lands[:, dst], T.slots[:, src]), dma="down")
    step("reload", "issued", lambda: sy.dma_start(T.finq[:, old:old + C].bitcast(u8), T.wc[:]),
         lambda: sy.dma_start(T.fins[:, old:old + C], T.ws[:]), dma="dfin")

    step("tu", "tc0", each(lambda half: ve.tensor_scalar(T.tu[half, :], T.tcw[lo, :], 2 * C - 1, None,
                                                         Op.bitwise_and), lo, hi))
    step("wl", "tu", lambda: ve.tensor_scalar(T.wl[:], T.tu[:], float(C - 1), None, Op.min))
    step("tz", "tu selo cl", lambda: ve.tensor_tensor(T.tz[:], T.tu[:].indirect(T.selo[:, 0:1]), T.cl[:], Op.min))
    step("off", "tz", lambda: ve.tensor_copy(T.off[:, 0:3], T.tz[:, 0:3]))
    step("scat", "off tab marks", lambda: ve.tensor_copy(T.tab[:].indirect(T.off[:, 0:3]), T.marks[:]))

    step("tm", "tu m2", lambda: ve.tensor_tensor(T.tm[:], T.tu[:], T.m2[:], Op.add))
    step("wl2", "tm", lambda: ve.tensor_scalar(T.wl2[:], T.tm[:], float(C), None, Op.min))
    step("look", "scat wl2", lambda: sc.activation(T.pv[:, 16:16 + ALL], T.tab[:, 0:C + 16].indirect(T.wl2[:]), Fn.Copy))
    step("pt", "look pad", each(lambda x, y, n: ve.transpose(T.pt[:, x:x + n], T.pv[:, y:y + n]),
                                (0, 16, ALL), (ALL, 0, ALL + 32)))
    step("tt", "scat", lambda: ve.transpose(T.tt[:], T.tab[:, 0:C]))
    step("x1", "tt", each(lambda k: ve.tensor_tensor(T.x1[:, 32 * k:32 * k + 32], T.tt[:, 8 * k:C:32],
                                                     T.tt[:, 8 * k + 16:C:32], Op.min), 0, 1))
    step("t1", "pt", lambda: ve.tensor_tensor(T.x1[:, 64:89], T.pt[:, 8::32], T.pt[:, 24::32], Op.min))
    step("x2", "x1 t1", lambda: ve.tensor_tensor(T.x2[lo, 0:89], T.x1[lo, 0:89], T.x1[hi, 0:89], Op.min))
    step("x3", "x2", lambda: ve.tensor_tensor(T.x3[q0, 0:89], T.x2[q0, 0:89], T.x2[q1, 0:89], Op.min))
    step("rep", "x3", each(lambda qk: sc.activation(T.rep[qk, 0:25], T.x3[q0, 64:89], Fn.Abs,
                                                    bias=float(sign * TURN - HALF)), *quads))

    def partners(k):
        w0 = window[HALF * k][0]
        ops = (-1.0, float(LAND), Op.mult, Op.add) if up else (float(w0), float(ALL - w0), Op.subtract, Op.min)
        return ve.tensor_scalar(T.pl[:, 16 * k:16 * k + 16], T.rep[:, 0:25].indirect(T.gof[:, 2 * k:2 * k + 1]), *ops)

    step("pl", "rep gof", each(partners, 0, 1))

    step("xt", "x3", lambda: ve.transpose(T.xt[q0, :], T.x3[q0, 0:64]))
    step("xe", "xt jw", each(lambda x, y, n: ve.tensor_tensor(T.xd[q0, x:x + n], T.xt[q0, y:y + n], T.jw[q0, y:y + n],
                                                              Op.min), (16, 0, 32), (0, 0, 16), (48, 16, 16)))
    step("xd2", "xe", each(lambda qk: sc.activation(T.xd[qk, :], T.xd[q0, :], Fn.Copy), *quads[1:]))
    step("xr", "xd2", lambda: ve.transpose(T.xr[:], T.xd[:]))
    step("finl", "xr", each(lambda e: ve.tensor_scalar(T.finl[:, e:64:2], T.xr[:, 32 * e:32 * e + 32], float(HALF), None,
                                                       Op.add), 0, 1))
    step("upd", "xt", lambda: ve.tensor_tensor(T.upd[q0, :], T.xt[q0, 0:32], T.xt[q0, 32:64], Op.add))
    step("up1", "upd", lambda: sc.activation(T.upa[q0, :], T.upd[q0, :], Fn.Relu, bias=sign * TURN + 1.0))
    step("up2", "up1", lambda: sc.activation(T.upb[q0, :], T.upa[q0, :], Fn.Relu, bias=2.0, scale=-1.0))
    step("up", "up2", lambda: sy.dma_start(T.up[:], T.upb[q0, :]), dma="dout")

    def partner(qn, out, win, a, x, n, cast=lambda v: v):
        (w0, w1), o = window[a], a // 12 + x // 16
        src = cast(win[:, w0:w1]).indirect(T.pl[:, o:o + n // 16])
        dst = cast(out[:, a + x:a + x + n])
        return ve.tensor_copy(dst, src) if qn == "v" else sc.activation(dst, src, Fn.Copy)

    for h, a in (("a", HALF), ("b", 0)):
        k = "1" if a == early else "2"
        n = HALF - CAP if a else HALF
        here = "arrec arres" if a == early else "arrlc arrls own"
        codes, scales = ("arrec", "arres") if a == early == HALF else ("arrec arrlc own", "arres arrls own")
        cut = ((0, n),)
        step("wc" + k, "wc wl", lambda a=a: pickc(T.wselq, a, HALF, T.wq, T.wl))
        step("ws" + k, "ws wl", lambda a=a: picks(T.wsels, a, HALF, T.wqs, T.wl))
        step("w" + k, "wc%s ws%s u0 u1 u2 u3" % (k, k),
             each(lambda b, a=a: prod(a, b, b, "wselq", "wsels", True, False), 0, 1, 2, 3))
        step("o" + k, "u4 u5 u6 u7 " + here,
             each(lambda b, a=a: prod(a, b, 4 + b, "landq", "lands", False, False), 0, 1, 2, 3))
        step("pc" + h, "pl zq " + codes,
             each(lambda x, n, a=a: partner("v", T.parq, T.landq, a, x, n, lambda v: v.bitcast(u32)), *cut))
        step("ps" + h, "pl zq " + scales, lambda a=a, c=cut[0]: partner("s", T.pars, T.lands, a, *c))
        step("pv" + h, "pl zq " + scales, lambda a=a, c=cut[-1]: partner("v", T.pars, T.lands, a, *c))

        def rest(b, a=a, n=n):
            ins = prod(a, b, 4 + b, "parq", "pars", False, not up, n)
            return prod(a, b, 4 + b, "landq", "lands", False, True, at=base) if up else ins

        step("m" + h, "u4 u5 u6 u7 pc%s ps%s" % (h, h) + (" pv" + h) * (len(cut) - 1),
             *[lambda b=b, f=rest: f(b) for b in range(4)])
        for b in range(4):
            out, on = T.h[:, 4 * a + b:4 * (a + HALF):4], "h%s%d" % (h, b)
            step(on, "m%s.%d" % (h, b), (lambda o=out, i=bank(a, b): ve.tensor_copy(o, i)) if on in order["v"].split()
                 else (lambda o=out, i=bank(a, b): sc.activation(o, i, Fn.Copy)))
        step("q" + h, " ".join("h%s%d" % (h, b) for b in range(4)),
             lambda a=a: ve.quantize_mx(T.finq[:, new + a:new + a + HALF], T.fins[:, new + a:new + a + HALF],
                                        T.h[:, 4 * a:4 * (a + HALF)]))

    runs = [(sum(PIECES[:i]), n) for i, n in enumerate(PIECES)]
    step("last", "qa qb finl reload", *[lambda a=a, n=n: pickc(T.outq, a, n, T.finq, T.finl) for a, n in runs])
    step("lasts", "qa qb finl reload", lambda: picks(T.outs, 0, C, T.fins, T.finl))

    def store(i):
        a, n = runs[i]
        wait("y", "last.%d" % i)
        return sy.dma_start(T.oc[:, 4 * a:4 * (a + n)], T.outq[:, a:a + n].bitcast(u8))

    step("oc", "", *[lambda i=i: store(i) for i in range(len(runs) - 1)], dma="dout")
    step("ocl", "", lambda: store(len(runs) - 1), dma="dout")
    for i, q in enumerate((sc, sy)):
        step("osc%d" % i, "lasts", *[lambda k=k, q=q: q.dma_start(T.osc[4 * k:4 * k + 4, :], T.outs[32 * k:32 * k + 4, :])
                                     for k in (i, i + 2)], dma="dout")

    cnt = {}
    for qn, names in order.items():
        for name in names.split():
            _needs, parts, dma = steps[name]
            if name != "send":
                for i in range(len(parts)):
                    s = dma or mine[qn]
                    cnt[s] = cnt.get(s, 0) + (16 if dma else 1)
                    done[name] = done["%s.%d" % (name, i)] = (s, cnt[s])
    for name, (_needs, _parts, dma) in steps.items():
        if dma:
            done[name] = (dma, cnt[dma])
    for qn, names in order.items():
        for name in names.split():
            needs, parts, dma = steps[name]
            for what in needs:
                wait(qn, what)
            for part in parts:
                ins = part()
                if name != "send":
                    ins.then_inc(sem[dma or mine[qn]], 16 if dma else 1)

    wait("g", "sent")
    for name in ("vec", "act", "ten", "gpc", "dout"):
        g.wait_ge(sem[name], cnt[name])
